import numpy as np
import ml_dtypes


def mxq(x, axis, fmt="e4m3"):
    dtype, down = {"e4m3": (ml_dtypes.float8_e4m3fn, 7), "e5m2": (ml_dtypes.float8_e5m2, 14)}[fmt]
    v = np.moveaxis(np.asarray(x, np.float32).astype(ml_dtypes.bfloat16).astype(np.float64), axis, -1)
    blocks = v.reshape(v.shape[:-1] + (-1, 32))
    amax = np.abs(blocks).max(-1, keepdims=True)
    byte = np.maximum(np.where(amax > 0, np.frexp(amax)[1] - 1 + 127, 0) - down, 1)
    scale = np.exp2(byte - 127.0)
    codes = (blocks / scale).astype(np.float32).astype(dtype).astype(np.float64)
    return np.moveaxis((codes * scale).reshape(v.shape), -1, axis)


WIDE = False


def mx_kscale(k):
    if not WIDE:
        return np.ones(k)
    levels = np.array([24, -24, 12, -12, 0])
    if k % 512:
        return np.exp2(np.random.permutation(np.resize(levels, k // 32))).repeat(32)
    a = np.empty((k // 512, 16))
    for p in range(k // 512):
        a[p, :8] = np.random.permutation(np.resize(levels, 8))
        for g in range(8):
            far = levels[np.abs(levels - a[p, g]) >= 10]
            a[p, g + 8] = far[np.random.randint(len(far))]
    return np.exp2(a.ravel()).repeat(32)


def f64(x):
    return np.asarray(x).astype(np.float64)


def striped(idx):
    return np.tile(idx.reshape(-1, 16).T, (8, 1)).astype(np.uint16)


def unstriped(offs):
    return offs[:16].T.reshape(-1).astype(np.int64)


E2M1 = np.array([0.0, 0.5, 1.0, 1.5, 2.0, 3.0, 4.0, 6.0, -0.0, -0.5, -1.0, -1.5, -2.0, -3.0, -4.0, -6.0])


def pack_weight(w, fmt):
    k, n = w.shape
    w = f64(np.asarray(w, np.float32).astype(ml_dtypes.bfloat16)).reshape(k // 32, 32, n)
    amax = np.abs(w).max(1)
    if fmt == "e4m3":
        byte = np.frexp(amax)[1] - 1 + 127 - 7
    else:
        mant, ex = np.frexp(amax / 6.0)
        byte = np.where(mant > 0.5, ex, ex - 1) + 127
    byte = np.clip(np.where(amax > 0, byte, 1), 1, 254)
    scaled = (w * np.exp2(127.0 - byte)[:, None, :]).reshape(k, n).astype(np.float32)
    by_word = np.ascontiguousarray(scaled.reshape(k // 512, 128, 4, n).transpose(0, 1, 3, 2))
    if fmt == "e4m3":
        words = by_word.astype(ml_dtypes.float8_e4m3fn).view(np.uint8)
    else:
        c = by_word.astype(ml_dtypes.float4_e2m1fn).view(np.uint8) & 0xF
        words = (c[..., 0::2] | (c[..., 1::2] << 4)).reshape(k // 512, 128, 2 * n)
    return np.ascontiguousarray(words), np.ascontiguousarray(byte.astype(np.uint8).reshape(k // 512, 16, n))


def unpack_weight(words, scales, fmt):
    g, _, n = scales.shape
    words = np.ascontiguousarray(words).reshape(g, 128, n, -1)
    if fmt == "e4m3":
        vals = words.view(ml_dtypes.float8_e4m3fn).astype(np.float64)
    else:
        nib = np.empty((g, 128, n, 4), np.uint8)
        nib[..., 0::2] = words & 0xF
        nib[..., 1::2] = words >> 4
        vals = E2M1[nib]
    vals = vals * np.repeat(np.exp2(scales.astype(np.float64) - 127.0), 8, axis=1)[..., None]
    return vals.transpose(0, 1, 3, 2).reshape(g * 512, n)


def split(x):
    m, e = np.frexp(f64(x))
    hi = np.ldexp(np.trunc(16.0 * m) / 16.0, e)
    return hi, f64(x) - hi


K, N, T, J = 1024, 256, 1024, 512


def setup_inputs():
    n = np.random.standard_normal
    s = mx_kscale(K)[:, None]
    p_tab = pack_weight(n((K, T)) * s, "e4m3")
    return {
        "tab_words": p_tab[0],
        "tab_scales": p_tab[1],
        "wk": (n((K, N)) / np.sqrt(K) / s).astype(np.float32),
        "wv": (n((K, N)) / np.sqrt(K) / s).astype(np.float32),
        "st": (n((N, J))).astype(np.float32),
        "rT": (n((N, T))).astype(np.float32),
        "offs": striped(np.random.permutation(T)[:J]),
    }


def reference(tab_words, tab_scales, wk, wv, st, rT, offs):
    idx = unstriped(offs)
    tab_ = unpack_weight(tab_words, tab_scales, "e4m3")[:, idx]
    wk_ = mxq(f64(wk), 0, "e4m3")
    wv_hi, wv_lo = split(wv)
    wv_hi_, wv_lo_ = mxq(wv_hi, 0, "e4m3"), mxq(wv_lo, 0, "e4m3")
    ke = wk_.T @ tab_
    ve = wv_hi_.T @ tab_ + wv_lo_.T @ tab_
    gate = np.tanh(ke * f64(st))
    return f64(rT)[:, idx] + gate * ve

@@ -1,0 +1,173 @@
+from contextlib import ExitStack
+
+import concourse.mybir as mybir
+
+K, N, T, J = 1024, 256, 1024, 512
+FLOPS = 2 * 3 * K * N * J
+
+F32 = mybir.dt.float32
+BF16 = mybir.dt.bfloat16
+I32 = mybir.dt.int32
+U32 = mybir.dt.uint32
+U16 = mybir.dt.uint16
+U8 = mybir.dt.uint8
+FP8X4 = mybir.dt.float8_e4m3fn_x4
+ALU = mybir.AluOpType
+ACT = mybir.ActivationFunctionType
+
+P = 128
+PACK = 4
+PASSES = K // (P * PACK)
+HALVES = N // P
+HI_MASK = 0xFFF0FFF0 - (1 << 32)
+
+
+def rows_walk(ap):
+    return ap.rearrange("p t (c i) -> p c t i", i=2)
+
+
+def packed_walk(ap):
+    return ap.rearrange("p (c i t) -> p c t i", i=2, t=PACK)
+
+
+def tile_list_engram_hl_tanhL_kernel(
+    tc, tab_words, tab_scales, wk, wv, st, rT, offs, out
+):
+    nc = tc.nc
+    with ExitStack() as ctx:
+        sb = ctx.enter_context(tc.tile_pool(name="sb", bufs=1))
+        ps = ctx.enter_context(tc.psum_pool(name="ps", bufs=1))
+
+        def tiles(name, count, shape, dtype):
+            return [sb.tile(shape, dtype, name=f"{name}{i}", align_bytes=64) for i in range(count)]
+
+        offsets = sb.tile([P, J // 16], U16, name="offsets")
+        tab_plane = sb.tile([P, T], U8, name="tab_plane", align_bytes=64)
+        picked_plane = sb.tile([P, J], U8, name="picked_plane", align_bytes=64)
+        warm = sb.tile([P, 8], F32, name="warm")
+        warm2 = sb.tile([P, 8], F32, name="warm2")
+        tab_w = tiles("tab_w", PASSES, [P, T], I32)
+        picked_w = tiles("picked_w", PASSES, [P, J], U32)
+        wk_raw = tiles("wk_raw", PASSES, [P, PACK, N], F32)
+        wv_raw = tiles("wv_raw", PASSES, [P, PACK, N], F32)
+        wk_bf = tiles("wk_bf", PASSES, [P, PACK * N], BF16)
+        wv_top = tiles("wv_top", PASSES, [P, PACK * N], BF16)
+        wv_bf = tiles("wv_bf", PASSES, [P, 2 * PACK * N], BF16)
+        wk_codes = tiles("wk_codes", PASSES, [P, N], U32)
+        wk_plane = tiles("wk_plane", PASSES, [P, N], U8)
+        wv_codes = tiles("wv_codes", PASSES, [P, 2 * N], U32)
+        wv_plane = tiles("wv_plane", PASSES, [P, 2 * N], U8)
+        st_sb = tiles("st_sb", HALVES, [P, J], F32)
+        r_sb = tiles("r_sb", HALVES, [P, T], F32)
+        z = tiles("z", HALVES, [P, J], F32)
+        gate = tiles("gate", HALVES, [P, J], F32)
+        prod = tiles("prod", HALVES, [P, J], F32)
+        res = tiles("res", HALVES, [P, J], F32)
+        ke = [ps.tile([P, J], F32, name=f"ke{h}") for h in range(HALVES)]
+        ve = [ps.tile([P, J], F32, name=f"ve{h}") for h in range(HALVES)]
+
+        def load_words(a):
+            nc.sync.dma_start(tab_w[a][:], tab_words[a].rearrange("p t i -> p (t i)").bitcast(I32))
+
+        def load_weight(dst, src, a):
+            rows = src[a * P * PACK : (a + 1) * P * PACK, :]
+            nc.sync.dma_start(dst[a][:], rows.rearrange("(p t) n -> p t n", t=PACK))
+
+        nc.vector.memset(tab_plane[:].bitcast(I32), 0)
+        nc.gpsimd.memset(warm[:], 0.0)
+        nc.scalar.activation(warm2[:], warm[:], ACT.Tanh)
+        nc.sync.dma_start(offsets[:], offs)
+        load_words(0)
+        for q in range(4):
+            nc.sync.dma_start(
+                tab_plane[32 * q : 32 * q + 4 * PASSES, :].bitcast(I32),
+                tab_scales[:, 4 * q : 4 * q + 4, :].bitcast(I32),
+            )
+        load_weight(wv_raw, wv, 0)
+        load_words(1)
+        load_weight(wv_raw, wv, 1)
+        load_weight(wk_raw, wk, 0)
+        load_weight(wk_raw, wk, 1)
+        for h in range(HALVES):
+            nc.sync.dma_start(st_sb[h][:], st[h * P : (h + 1) * P, :])
+        for h in range(HALVES):
+            nc.sync.dma_start(r_sb[h][:], rT[h * P : (h + 1) * P, :])
+
+        def gather_words(a):
+            nc.vector.tensor_copy(picked_w[a][:], tab_w[a][:].bitcast(U32).indirect(offsets[:]))
+
+        def take_top(a):
+            halves = wv_raw[a][:].bitcast(BF16).rearrange("p t (c i e) -> p c t i e", i=2, e=2)
+            nc.scalar.copy(packed_walk(wv_top[a][:]), halves[:, :, :, :, 1])
+
+        def cast_wk(a):
+            nc.scalar.copy(packed_walk(wk_bf[a][:]), rows_walk(wk_raw[a][:]))
+
+        def mask_hi(a):
+            nc.vector.tensor_scalar(
+                wv_bf[a][:, : PACK * N].bitcast(I32),
+                wv_top[a][:].bitcast(I32),
+                HI_MASK,
+                None,
+                ALU.bitwise_and,
+            )
+
+        def make_lo(a):
+            nc.vector.tensor_tensor(
+                packed_walk(wv_bf[a][:, PACK * N :]),
+                rows_walk(wv_raw[a][:]),
+                packed_walk(wv_bf[a][:, : PACK * N]),
+                ALU.subtract,
+            )
+
+        def quantise(codes, plane, src):
+            nc.vector.quantize_mx(out=codes[:].bitcast(FP8X4), scales=plane[:], in_=src[:])
+
+        def mx_pass(acc, codes, plane, col, a, start, stop):
+            nc.tensor.matmul_mx(
+                out=acc[:],
+                lhsT=codes[:, col : col + P].bitcast(FP8X4),
+                lhsT_scale=plane[:, col : col + P],
+                rhs=picked_w[a][:].bitcast(FP8X4),
+                rhs_scale=picked_plane[4 * a : P, :],
+                start=start,
+                stop=stop,
+            )
+
+        def ve_passes(a):
+            for h in range(HALVES):
+                mx_pass(ve[h], wv_codes[a], wv_plane[a], h * P, a, a == 0, False)
+                mx_pass(ve[h], wv_codes[a], wv_plane[a], N + h * P, a, False, a == PASSES - 1)
+
+        def ke_passes(a):
+            for h in range(HALVES):
+                mx_pass(ke[h], wk_codes[a], wk_plane[a], h * P, a, a == 0, a == PASSES - 1)
+
+        gather_words(0)
+        nc.vector.tensor_copy(picked_plane[:], tab_plane[:].indirect(offsets[:]))
+        take_top(0)
+        gather_words(1)
+        take_top(1)
+        cast_wk(0)
+        cast_wk(1)
+        mask_hi(0)
+        make_lo(0)
+        mask_hi(1)
+        quantise(wv_codes[0], wv_plane[0], wv_bf[0])
+        ve_passes(0)
+        make_lo(1)
+        quantise(wk_codes[0], wk_plane[0], wk_bf[0])
+        ke_passes(0)
+        quantise(wv_codes[1], wv_plane[1], wv_bf[1])
+        quantise(wk_codes[1], wk_plane[1], wk_bf[1])
+        ke_passes(1)
+        ve_passes(1)
+
+        for h in range(HALVES):
+            nc.vector.tensor_tensor(z[h][:], ke[h][:], st_sb[h][:], ALU.mult)
+            nc.scalar.activation(gate[h][:], z[h][:], ACT.Tanh)
+        for h in range(HALVES):
+            nc.vector.tensor_tensor(prod[h][:], ve[h][:], gate[h][:], ALU.mult)
+        for h in range(HALVES):
+            nc.vector.tensor_tensor(res[h][:], r_sb[h][:].indirect(offsets[:]), prod[h][:], ALU.add)
+            nc.sync.dma_start(out[h * P : (h + 1) * P, :], res[h][:])

@@ -19,7 +19,7 @@ P = 128
 PACK = 4
 PASSES = K // (P * PACK)
 HALVES = N // P
-HI_MASK = 0xFFF0FFF0 - (1 << 32)
+HI_MASK = 0xFFF00000 - (1 << 32)
 
 
 def rows_walk(ap):
@@ -51,7 +51,7 @@ def tile_list_engram_hl_tanhL_kernel(
         wk_raw = tiles("wk_raw", PASSES, [P, PACK, N], F32)
         wv_raw = tiles("wv_raw", PASSES, [P, PACK, N], F32)
         wk_bf = tiles("wk_bf", PASSES, [P, PACK * N], BF16)
-        wv_top = tiles("wv_top", PASSES, [P, PACK * N], BF16)
+        wv_hi = tiles("wv_hi", PASSES, [P, PACK, N], F32)
         wv_bf = tiles("wv_bf", PASSES, [P, 2 * PACK * N], BF16)
         wk_codes = tiles("wk_codes", PASSES, [P, N], U32)
         wk_plane = tiles("wk_plane", PASSES, [P, N], U8)
@@ -84,44 +84,51 @@ def tile_list_engram_hl_tanhL_kernel(
                 tab_scales[:, 4 * q : 4 * q + 4, :].bitcast(I32),
             )
         load_weight(wv_raw, wv, 0)
-        load_words(1)
-        load_weight(wv_raw, wv, 1)
         load_weight(wk_raw, wk, 0)
+        load_words(1)
         load_weight(wk_raw, wk, 1)
-        for h in range(HALVES):
-            nc.sync.dma_start(st_sb[h][:], st[h * P : (h + 1) * P, :])
-        for h in range(HALVES):
-            nc.sync.dma_start(r_sb[h][:], rT[h * P : (h + 1) * P, :])
+        load_weight(wv_raw, wv, 1)
+        nc.sync.dma_start(st_sb[0][:], st[0:P, :])
+        nc.sync.dma_start(st_sb[1][:], st[P:N, :])
+        nc.sync.dma_start(r_sb[0][:], rT[0:P, :])
+        nc.sync.dma_start(r_sb[1][:], rT[P:N, :])
 
         def gather_words(a):
             nc.vector.tensor_copy(picked_w[a][:], tab_w[a][:].bitcast(U32).indirect(offsets[:]))
 
-        def take_top(a):
-            halves = wv_raw[a][:].bitcast(BF16).rearrange("p t (c i e) -> p c t i e", i=2, e=2)
-            nc.scalar.copy(packed_walk(wv_top[a][:]), halves[:, :, :, :, 1])
+        W = PACK * P
 
-        def cast_wk(a):
-            nc.scalar.copy(packed_walk(wk_bf[a][:]), rows_walk(wk_raw[a][:]))
+        def cast_hi(a, h0, h1):
+            dst = wv_bf[a][:].rearrange("p (h s c i t) -> p h s c t i", h=HALVES, s=2, i=2, t=PACK)
+            for h in range(h0, h1):
+                nc.scalar.copy(dst[:, h, 0], rows_walk(wv_hi[a][:, :, h * P : (h + 1) * P]))
+
+        def cast_wk(a, h0, h1):
+            nc.scalar.copy(packed_walk(wk_bf[a][:, h0 * W : h1 * W]), rows_walk(wk_raw[a][:, :, h0 * P : h1 * P]))
 
         def mask_hi(a):
             nc.vector.tensor_scalar(
-                wv_bf[a][:, : PACK * N].bitcast(I32),
-                wv_top[a][:].bitcast(I32),
-                HI_MASK,
-                None,
-                ALU.bitwise_and,
+                wv_hi[a][:].bitcast(I32), wv_raw[a][:].bitcast(I32), HI_MASK, None, ALU.bitwise_and
             )
 
-        def make_lo(a):
+        def make_lo(a, h):
             nc.vector.tensor_tensor(
-                packed_walk(wv_bf[a][:, PACK * N :]),
-                rows_walk(wv_raw[a][:]),
-                packed_walk(wv_bf[a][:, : PACK * N]),
+                packed_walk(wv_bf[a][:, (2 * h + 1) * W : (2 * h + 2) * W]),
+                rows_walk(wv_raw[a][:, :, h * P : (h + 1) * P]),
+                rows_walk(wv_hi[a][:, :, h * P : (h + 1) * P]),
                 ALU.subtract,
             )
 
-        def quantise(codes, plane, src):
-            nc.vector.quantize_mx(out=codes[:].bitcast(FP8X4), scales=plane[:], in_=src[:])
+        def quantise(codes, plane, src, c0, c1):
+            nc.vector.quantize_mx(
+                out=codes[:, c0 * P : c1 * P].bitcast(FP8X4), scales=plane[:, c0 * P : c1 * P], in_=src[:, c0 * W : c1 * W]
+            )
+
+        def q_wv(a, h0, h1):
+            quantise(wv_codes[a], wv_plane[a], wv_bf[a], 2 * h0, 2 * h1)
+
+        def q_wk(a, h0, h1):
+            quantise(wk_codes[a], wk_plane[a], wk_bf[a], h0, h1)
 
         def mx_pass(acc, codes, plane, col, a, start, stop):
             nc.tensor.matmul_mx(
@@ -134,40 +141,60 @@ def tile_list_engram_hl_tanhL_kernel(
                 stop=stop,
             )
 
-        def ve_passes(a):
-            for h in range(HALVES):
-                mx_pass(ve[h], wv_codes[a], wv_plane[a], h * P, a, a == 0, False)
-                mx_pass(ve[h], wv_codes[a], wv_plane[a], N + h * P, a, False, a == PASSES - 1)
+        def ve_passes(a, h):
+            mx_pass(ve[h], wv_codes[a], wv_plane[a], 2 * h * P, a, a == 0, False)
+            mx_pass(ve[h], wv_codes[a], wv_plane[a], (2 * h + 1) * P, a, False, a == PASSES - 1)
 
-        def ke_passes(a):
-            for h in range(HALVES):
-                mx_pass(ke[h], wk_codes[a], wk_plane[a], h * P, a, a == 0, a == PASSES - 1)
+        def ke_pass(a, h):
+            mx_pass(ke[h], wk_codes[a], wk_plane[a], h * P, a, a == 0, a == PASSES - 1)
 
-        gather_words(0)
-        nc.vector.tensor_copy(picked_plane[:], tab_plane[:].indirect(offsets[:]))
-        take_top(0)
-        gather_words(1)
-        take_top(1)
-        cast_wk(0)
-        cast_wk(1)
-        mask_hi(0)
-        make_lo(0)
-        mask_hi(1)
-        quantise(wv_codes[0], wv_plane[0], wv_bf[0])
-        ve_passes(0)
-        make_lo(1)
-        quantise(wk_codes[0], wk_plane[0], wk_bf[0])
-        ke_passes(0)
-        quantise(wv_codes[1], wv_plane[1], wv_bf[1])
-        quantise(wk_codes[1], wk_plane[1], wk_bf[1])
-        ke_passes(1)
-        ve_passes(1)
-
-        for h in range(HALVES):
+        def gate_of(h):
             nc.vector.tensor_tensor(z[h][:], ke[h][:], st_sb[h][:], ALU.mult)
             nc.scalar.activation(gate[h][:], z[h][:], ACT.Tanh)
-        for h in range(HALVES):
+
+        def gated(h):
             nc.vector.tensor_tensor(prod[h][:], ve[h][:], gate[h][:], ALU.mult)
-        for h in range(HALVES):
-            nc.vector.tensor_tensor(res[h][:], r_sb[h][:].indirect(offsets[:]), prod[h][:], ALU.add)
-            nc.sync.dma_start(out[h * P : (h + 1) * P, :], res[h][:])
+
+        def finish(h, j0, j1):
+            nc.vector.tensor_tensor(
+                res[h][:, j0:j1], r_sb[h][:].indirect(offsets[:, j0 // 16 : j1 // 16]), prod[h][:, j0:j1], ALU.add
+            )
+            nc.sync.dma_start(out[h * P : (h + 1) * P, j0:j1], res[h][:, j0:j1])
+
+        def gather_scales():
+            nc.vector.tensor_copy(picked_plane[:], tab_plane[:].indirect(offsets[:]))
+
+        gather_words(0)
+        mask_hi(0)
+        cast_hi(0, 0, 2)
+        cast_wk(0, 0, 2)
+        gather_scales()
+        make_lo(0, 0)
+        make_lo(0, 1)
+        q_wk(0, 0, 2)
+        q_wv(0, 0, 1)
+        q_wv(0, 1, 2)
+        gather_words(1)
+        ke_pass(0, 0)
+        ke_pass(0, 1)
+        ve_passes(0, 0)
+        ve_passes(0, 1)
+        cast_wk(1, 0, 2)
+        mask_hi(1)
+        cast_hi(1, 0, 2)
+        q_wk(1, 0, 2)
+        ke_pass(1, 0)
+        ke_pass(1, 1)
+        make_lo(1, 0)
+        make_lo(1, 1)
+        q_wv(1, 0, 1)
+        ve_passes(1, 0)
+        gate_of(0)
+        q_wv(1, 1, 2)
+        ve_passes(1, 1)
+        gate_of(1)
+        gated(0)
+        gated(1)
+        finish(0, 0, J)
+        finish(1, 0, 384)
+        finish(1, 384, J)

@@ -19,7 +19,12 @@ P = 128
 PACK = 4
 PASSES = K // (P * PACK)
 HALVES = N // P
+W = PACK * P
 HI_MASK = 0xFFF00000 - (1 << 32)
+HI_MASK_PAIR = 0xFFF0FFF0 - (1 << 32)
+HI = (2, 4)
+LO = (3, 5)
+KEY = (0, 1)
 
 
 def rows_walk(ap):
@@ -50,13 +55,11 @@ def tile_list_engram_hl_tanhL_kernel(
         picked_w = tiles("picked_w", PASSES, [P, J], U32)
         wk_raw = tiles("wk_raw", PASSES, [P, PACK, N], F32)
         wv_raw = tiles("wv_raw", PASSES, [P, PACK, N], F32)
-        wk_bf = tiles("wk_bf", PASSES, [P, PACK * N], BF16)
         wv_hi = tiles("wv_hi", PASSES, [P, PACK, N], F32)
-        wv_bf = tiles("wv_bf", PASSES, [P, 2 * PACK * N], BF16)
-        wk_codes = tiles("wk_codes", PASSES, [P, N], U32)
-        wk_plane = tiles("wk_plane", PASSES, [P, N], U8)
-        wv_codes = tiles("wv_codes", PASSES, [P, 2 * N], U32)
-        wv_plane = tiles("wv_plane", PASSES, [P, 2 * N], U8)
+        wv_top = sb.tile([P, PACK * N], BF16, name="wv_top")
+        w_bf = tiles("w_bf", PASSES, [P, 6 * W], BF16)
+        w_codes = tiles("w_codes", PASSES, [P, 6 * P], U32)
+        w_plane = tiles("w_plane", PASSES, [P, 6 * P], U8)
         st_sb = tiles("st_sb", HALVES, [P, J], F32)
         r_sb = tiles("r_sb", HALVES, [P, T], F32)
         z = tiles("z", HALVES, [P, J], F32)
@@ -73,68 +76,79 @@ def tile_list_engram_hl_tanhL_kernel(
             rows = src[a * P * PACK : (a + 1) * P * PACK, :]
             nc.sync.dma_start(dst[a][:], rows.rearrange("(p t) n -> p t n", t=PACK))
 
-        nc.vector.memset(tab_plane[:].bitcast(I32), 0)
-        nc.gpsimd.memset(warm[:], 0.0)
-        nc.scalar.activation(warm2[:], warm[:], ACT.Tanh)
-        nc.sync.dma_start(offsets[:], offs)
-        load_words(0)
-        for q in range(4):
-            nc.sync.dma_start(
-                tab_plane[32 * q : 32 * q + 4 * PASSES, :].bitcast(I32),
-                tab_scales[:, 4 * q : 4 * q + 4, :].bitcast(I32),
-            )
-        load_weight(wv_raw, wv, 0)
-        load_weight(wk_raw, wk, 0)
-        load_words(1)
-        load_weight(wk_raw, wk, 1)
-        load_weight(wv_raw, wv, 1)
-        nc.sync.dma_start(st_sb[0][:], st[0:P, :])
-        nc.sync.dma_start(st_sb[1][:], st[P:N, :])
-        nc.sync.dma_start(r_sb[0][:], rT[0:P, :])
-        nc.sync.dma_start(r_sb[1][:], rT[P:N, :])
+        def load_scales():
+            for q in range(4):
+                nc.sync.dma_start(
+                    tab_plane[32 * q : 32 * q + 4 * PASSES, :].bitcast(I32),
+                    tab_scales[:, 4 * q : 4 * q + 4, :].bitcast(I32),
+                )
+
+        def slot(a, s, n=1):
+            return w_bf[a][:, s * W : (s + n) * W]
+
+        def half(t3, h):
+            return t3[:, :, h * P : (h + 1) * P]
 
         def gather_words(a):
             nc.vector.tensor_copy(picked_w[a][:], tab_w[a][:].bitcast(U32).indirect(offsets[:]))
 
-        W = PACK * P
+        def gather_scales():
+            nc.vector.tensor_copy(picked_plane[:], tab_plane[:].indirect(offsets[:]))
 
-        def cast_hi(a, h0, h1):
-            dst = wv_bf[a][:].rearrange("p (h s c i t) -> p h s c t i", h=HALVES, s=2, i=2, t=PACK)
-            for h in range(h0, h1):
-                nc.scalar.copy(dst[:, h, 0], rows_walk(wv_hi[a][:, :, h * P : (h + 1) * P]))
+        def cast_wk(a):
+            nc.scalar.copy(packed_walk(slot(a, 0, 2)), rows_walk(wk_raw[a][:]))
 
-        def cast_wk(a, h0, h1):
-            nc.scalar.copy(packed_walk(wk_bf[a][:, h0 * W : h1 * W]), rows_walk(wk_raw[a][:, :, h0 * P : h1 * P]))
-
-        def mask_hi(a):
+        def mask_hi(a, h):
             nc.vector.tensor_scalar(
-                wv_hi[a][:].bitcast(I32), wv_raw[a][:].bitcast(I32), HI_MASK, None, ALU.bitwise_and
+                half(wv_hi[a], h).bitcast(I32), half(wv_raw[a], h).bitcast(I32), HI_MASK, None, ALU.bitwise_and
             )
+
+        def cast_hi(a, h):
+            nc.scalar.copy(packed_walk(slot(a, HI[h])), rows_walk(half(wv_hi[a], h)))
 
         def make_lo(a, h):
             nc.vector.tensor_tensor(
-                packed_walk(wv_bf[a][:, (2 * h + 1) * W : (2 * h + 2) * W]),
-                rows_walk(wv_raw[a][:, :, h * P : (h + 1) * P]),
-                rows_walk(wv_hi[a][:, :, h * P : (h + 1) * P]),
+                packed_walk(slot(a, LO[h])), rows_walk(half(wv_raw[a], h)), rows_walk(half(wv_hi[a], h)), ALU.subtract
+            )
+
+        def make_lo_pool(a, h):
+            nc.gpsimd.tensor_tensor(
+                slot(a, LO[h]).rearrange("p (n t) -> p n t", t=PACK),
+                half(wv_raw[a], h).rearrange("p t n -> p n t"),
+                half(wv_hi[a], h).rearrange("p t n -> p n t"),
                 ALU.subtract,
             )
 
-        def quantise(codes, plane, src, c0, c1):
-            nc.vector.quantize_mx(
-                out=codes[:, c0 * P : c1 * P].bitcast(FP8X4), scales=plane[:, c0 * P : c1 * P], in_=src[:, c0 * W : c1 * W]
+        def take_top(a):
+            halves = wv_raw[a][:].bitcast(BF16).rearrange("p t (c i e) -> p c t i e", i=2, e=2)
+            nc.scalar.copy(packed_walk(wv_top[:]), halves[:, :, :, :, 1])
+
+        def mask_top(a):
+            nc.vector.tensor_scalar(
+                slot(a, 2, 4).bitcast(I32).rearrange("p (h s w) -> p h s w", h=HALVES, s=2)[:, :, 0, :],
+                wv_top[:].bitcast(I32).rearrange("p (h w) -> p h w", h=HALVES),
+                HI_MASK_PAIR,
+                None,
+                ALU.bitwise_and,
             )
 
-        def q_wv(a, h0, h1):
-            quantise(wv_codes[a], wv_plane[a], wv_bf[a], 2 * h0, 2 * h1)
+        def make_lo_top(a, h):
+            nc.vector.tensor_tensor(
+                packed_walk(slot(a, LO[h])), rows_walk(half(wv_raw[a], h)), packed_walk(slot(a, HI[h])), ALU.subtract
+            )
 
-        def q_wk(a, h0, h1):
-            quantise(wk_codes[a], wk_plane[a], wk_bf[a], h0, h1)
+        def quantise(a, s, n):
+            nc.vector.quantize_mx(
+                out=w_codes[a][:, s * P : (s + n) * P].bitcast(FP8X4),
+                scales=w_plane[a][:, s * P : (s + n) * P],
+                in_=slot(a, s, n),
+            )
 
-        def mx_pass(acc, codes, plane, col, a, start, stop):
+        def mx_pass(acc, a, s, start, stop):
             nc.tensor.matmul_mx(
                 out=acc[:],
-                lhsT=codes[:, col : col + P].bitcast(FP8X4),
-                lhsT_scale=plane[:, col : col + P],
+                lhsT=w_codes[a][:, s * P : (s + 1) * P].bitcast(FP8X4),
+                lhsT_scale=w_plane[a][:, s * P : (s + 1) * P],
                 rhs=picked_w[a][:].bitcast(FP8X4),
                 rhs_scale=picked_plane[4 * a : P, :],
                 start=start,
@@ -142,11 +156,11 @@ def tile_list_engram_hl_tanhL_kernel(
             )
 
         def ve_passes(a, h):
-            mx_pass(ve[h], wv_codes[a], wv_plane[a], 2 * h * P, a, a == 0, False)
-            mx_pass(ve[h], wv_codes[a], wv_plane[a], (2 * h + 1) * P, a, False, a == PASSES - 1)
+            mx_pass(ve[h], a, HI[h], a == 0, False)
+            mx_pass(ve[h], a, LO[h], False, a == PASSES - 1)
 
         def ke_pass(a, h):
-            mx_pass(ke[h], wk_codes[a], wk_plane[a], h * P, a, a == 0, a == PASSES - 1)
+            mx_pass(ke[h], a, KEY[h], a == 0, a == PASSES - 1)
 
         def gate_of(h):
             nc.vector.tensor_tensor(z[h][:], ke[h][:], st_sb[h][:], ALU.mult)
@@ -161,36 +175,53 @@ def tile_list_engram_hl_tanhL_kernel(
             )
             nc.sync.dma_start(out[h * P : (h + 1) * P, j0:j1], res[h][:, j0:j1])
 
-        def gather_scales():
-            nc.vector.tensor_copy(picked_plane[:], tab_plane[:].indirect(offsets[:]))
+        nc.vector.memset(tab_plane[:].bitcast(I32), 0)
+        nc.gpsimd.memset(warm[:], 0.0)
+        nc.scalar.activation(warm2[:], warm[:], ACT.Tanh)
+        load_words(0)
+        nc.sync.dma_start(offsets[:], offs)
+        load_weight(wv_raw, wv, 0)
+        load_scales()
+        load_weight(wk_raw, wk, 0)
+        load_words(1)
+        load_weight(wk_raw, wk, 1)
+        load_weight(wv_raw, wv, 1)
+        nc.sync.dma_start(st_sb[0][:], st[0:P, :])
+        nc.sync.dma_start(st_sb[1][:], st[P:N, :])
+        nc.sync.dma_start(r_sb[0][:], rT[0:P, :])
+        nc.sync.dma_start(r_sb[1][:], rT[P:N, :])
 
         gather_words(0)
-        mask_hi(0)
-        cast_hi(0, 0, 2)
-        cast_wk(0, 0, 2)
+        mask_hi(0, 0)
+        mask_hi(0, 1)
+        cast_hi(0, 0)
+        cast_hi(0, 1)
+        cast_wk(0)
         gather_scales()
         make_lo(0, 0)
         make_lo(0, 1)
-        q_wk(0, 0, 2)
-        q_wv(0, 0, 1)
-        q_wv(0, 1, 2)
+        quantise(0, 0, 2)
+        quantise(0, 2, 2)
+        quantise(0, 4, 2)
         gather_words(1)
         ke_pass(0, 0)
         ke_pass(0, 1)
         ve_passes(0, 0)
         ve_passes(0, 1)
-        cast_wk(1, 0, 2)
-        mask_hi(1)
-        cast_hi(1, 0, 2)
-        q_wk(1, 0, 2)
+        cast_wk(1)
+        mask_hi(1, 0)
+        mask_hi(1, 1)
+        cast_hi(1, 0)
+        cast_hi(1, 1)
+        quantise(1, 0, 2)
         ke_pass(1, 0)
         ke_pass(1, 1)
         make_lo(1, 0)
         make_lo(1, 1)
-        q_wv(1, 0, 1)
+        quantise(1, 2, 2)
         ve_passes(1, 0)
         gate_of(0)
-        q_wv(1, 1, 2)
+        quantise(1, 4, 2)
         ve_passes(1, 1)
         gate_of(1)
         gated(0)

@@ -19,20 +19,27 @@ P = 128
 PACK = 4
 PASSES = K // (P * PACK)
 HALVES = N // P
-W = PACK * P
+QUADRANTS = 4
+SCALE_ROWS = 4
+PER_COLUMN = 16
+
 HI_MASK = 0xFFF00000 - (1 << 32)
-HI_MASK_PAIR = 0xFFF0FFF0 - (1 << 32)
+
+SLOTS = 6
+KEY = (0, 1)
 HI = (2, 4)
 LO = (3, 5)
-KEY = (0, 1)
+SLOT_VALUES = PACK * P
+
+LAST_CUT = 384
 
 
-def rows_walk(ap):
-    return ap.rearrange("p t (c i) -> p c t i", i=2)
+def rows_walk(rows):
+    return rows.rearrange("p t (c i) -> p c t i", i=2)
 
 
-def packed_walk(ap):
-    return ap.rearrange("p (c i t) -> p c t i", i=2, t=PACK)
+def packed_walk(values):
+    return values.rearrange("p (c i t) -> p c t i", i=2, t=PACK)
 
 
 def tile_list_engram_hl_tanhL_kernel(
@@ -46,20 +53,17 @@ def tile_list_engram_hl_tanhL_kernel(
         def tiles(name, count, shape, dtype):
             return [sb.tile(shape, dtype, name=f"{name}{i}", align_bytes=64) for i in range(count)]
 
-        offsets = sb.tile([P, J // 16], U16, name="offsets")
+        offsets = sb.tile([P, J // PER_COLUMN], U16, name="offsets")
         tab_plane = sb.tile([P, T], U8, name="tab_plane", align_bytes=64)
         picked_plane = sb.tile([P, J], U8, name="picked_plane", align_bytes=64)
-        warm = sb.tile([P, 8], F32, name="warm")
-        warm2 = sb.tile([P, 8], F32, name="warm2")
         tab_w = tiles("tab_w", PASSES, [P, T], I32)
         picked_w = tiles("picked_w", PASSES, [P, J], U32)
         wk_raw = tiles("wk_raw", PASSES, [P, PACK, N], F32)
         wv_raw = tiles("wv_raw", PASSES, [P, PACK, N], F32)
         wv_hi = tiles("wv_hi", PASSES, [P, PACK, N], F32)
-        wv_top = sb.tile([P, PACK * N], BF16, name="wv_top")
-        w_bf = tiles("w_bf", PASSES, [P, 6 * W], BF16)
-        w_codes = tiles("w_codes", PASSES, [P, 6 * P], U32)
-        w_plane = tiles("w_plane", PASSES, [P, 6 * P], U8)
+        w_bf = tiles("w_bf", PASSES, [P, SLOTS * SLOT_VALUES], BF16)
+        w_codes = tiles("w_codes", PASSES, [P, SLOTS * P], U32)
+        w_plane = tiles("w_plane", PASSES, [P, SLOTS * P], U8)
         st_sb = tiles("st_sb", HALVES, [P, J], F32)
         r_sb = tiles("r_sb", HALVES, [P, T], F32)
         z = tiles("z", HALVES, [P, J], F32)
@@ -77,17 +81,17 @@ def tile_list_engram_hl_tanhL_kernel(
             nc.sync.dma_start(dst[a][:], rows.rearrange("(p t) n -> p t n", t=PACK))
 
         def load_scales():
-            for q in range(4):
+            for quad in range(QUADRANTS):
                 nc.sync.dma_start(
-                    tab_plane[32 * q : 32 * q + 4 * PASSES, :].bitcast(I32),
-                    tab_scales[:, 4 * q : 4 * q + 4, :].bitcast(I32),
+                    tab_plane[32 * quad : 32 * quad + SCALE_ROWS * PASSES, :].bitcast(I32),
+                    tab_scales[:, SCALE_ROWS * quad : SCALE_ROWS * (quad + 1), :].bitcast(I32),
                 )
 
-        def slot(a, s, n=1):
-            return w_bf[a][:, s * W : (s + n) * W]
+        def slots(a, first, count=1):
+            return w_bf[a][:, first * SLOT_VALUES : (first + count) * SLOT_VALUES]
 
-        def half(t3, h):
-            return t3[:, :, h * P : (h + 1) * P]
+        def half(rows, h):
+            return rows[:, :, h * P : (h + 1) * P]
 
         def gather_words(a):
             nc.vector.tensor_copy(picked_w[a][:], tab_w[a][:].bitcast(U32).indirect(offsets[:]))
@@ -96,7 +100,7 @@ def tile_list_engram_hl_tanhL_kernel(
             nc.vector.tensor_copy(picked_plane[:], tab_plane[:].indirect(offsets[:]))
 
         def cast_wk(a):
-            nc.scalar.copy(packed_walk(slot(a, 0, 2)), rows_walk(wk_raw[a][:]))
+            nc.scalar.copy(packed_walk(slots(a, KEY[0], HALVES)), rows_walk(wk_raw[a][:]))
 
         def mask_hi(a, h):
             nc.vector.tensor_scalar(
@@ -104,80 +108,61 @@ def tile_list_engram_hl_tanhL_kernel(
             )
 
         def cast_hi(a, h):
-            nc.scalar.copy(packed_walk(slot(a, HI[h])), rows_walk(half(wv_hi[a], h)))
+            nc.scalar.copy(packed_walk(slots(a, HI[h])), rows_walk(half(wv_hi[a], h)))
 
         def make_lo(a, h):
             nc.vector.tensor_tensor(
-                packed_walk(slot(a, LO[h])), rows_walk(half(wv_raw[a], h)), rows_walk(half(wv_hi[a], h)), ALU.subtract
-            )
-
-        def make_lo_pool(a, h):
-            nc.gpsimd.tensor_tensor(
-                slot(a, LO[h]).rearrange("p (n t) -> p n t", t=PACK),
-                half(wv_raw[a], h).rearrange("p t n -> p n t"),
-                half(wv_hi[a], h).rearrange("p t n -> p n t"),
+                packed_walk(slots(a, LO[h])),
+                rows_walk(half(wv_raw[a], h)),
+                rows_walk(half(wv_hi[a], h)),
                 ALU.subtract,
             )
 
-        def take_top(a):
-            halves = wv_raw[a][:].bitcast(BF16).rearrange("p t (c i e) -> p c t i e", i=2, e=2)
-            nc.scalar.copy(packed_walk(wv_top[:]), halves[:, :, :, :, 1])
-
-        def mask_top(a):
-            nc.vector.tensor_scalar(
-                slot(a, 2, 4).bitcast(I32).rearrange("p (h s w) -> p h s w", h=HALVES, s=2)[:, :, 0, :],
-                wv_top[:].bitcast(I32).rearrange("p (h w) -> p h w", h=HALVES),
-                HI_MASK_PAIR,
-                None,
-                ALU.bitwise_and,
-            )
-
-        def make_lo_top(a, h):
-            nc.vector.tensor_tensor(
-                packed_walk(slot(a, LO[h])), rows_walk(half(wv_raw[a], h)), packed_walk(slot(a, HI[h])), ALU.subtract
-            )
-
-        def quantise(a, s, n):
+        def quantise_pair(a, first):
             nc.vector.quantize_mx(
-                out=w_codes[a][:, s * P : (s + n) * P].bitcast(FP8X4),
-                scales=w_plane[a][:, s * P : (s + n) * P],
-                in_=slot(a, s, n),
+                out=w_codes[a][:, first * P : (first + 2) * P].bitcast(FP8X4),
+                scales=w_plane[a][:, first * P : (first + 2) * P],
+                in_=slots(a, first, 2),
             )
 
-        def mx_pass(acc, a, s, start, stop):
+        def quantise_wk(a):
+            quantise_pair(a, KEY[0])
+
+        def quantise_wv(a, h):
+            quantise_pair(a, HI[h])
+
+        def mx_pass(acc, a, slot, start, stop):
             nc.tensor.matmul_mx(
                 out=acc[:],
-                lhsT=w_codes[a][:, s * P : (s + 1) * P].bitcast(FP8X4),
-                lhsT_scale=w_plane[a][:, s * P : (s + 1) * P],
+                lhsT=w_codes[a][:, slot * P : (slot + 1) * P].bitcast(FP8X4),
+                lhsT_scale=w_plane[a][:, slot * P : (slot + 1) * P],
                 rhs=picked_w[a][:].bitcast(FP8X4),
-                rhs_scale=picked_plane[4 * a : P, :],
+                rhs_scale=picked_plane[SCALE_ROWS * a : P, :],
                 start=start,
                 stop=stop,
             )
+
+        def ke_pass(a, h):
+            mx_pass(ke[h], a, KEY[h], a == 0, a == PASSES - 1)
 
         def ve_passes(a, h):
             mx_pass(ve[h], a, HI[h], a == 0, False)
             mx_pass(ve[h], a, LO[h], False, a == PASSES - 1)
 
-        def ke_pass(a, h):
-            mx_pass(ke[h], a, KEY[h], a == 0, a == PASSES - 1)
-
-        def gate_of(h):
+        def make_gate(h):
             nc.vector.tensor_tensor(z[h][:], ke[h][:], st_sb[h][:], ALU.mult)
             nc.scalar.activation(gate[h][:], z[h][:], ACT.Tanh)
 
-        def gated(h):
+        def apply_gate(h):
             nc.vector.tensor_tensor(prod[h][:], ve[h][:], gate[h][:], ALU.mult)
 
-        def finish(h, j0, j1):
-            nc.vector.tensor_tensor(
-                res[h][:, j0:j1], r_sb[h][:].indirect(offsets[:, j0 // 16 : j1 // 16]), prod[h][:, j0:j1], ALU.add
-            )
+        def add_record_and_store(h, j0, j1):
+            entries = offsets[:, j0 // PER_COLUMN : j1 // PER_COLUMN]
+            nc.vector.tensor_tensor(res[h][:, j0:j1], r_sb[h][:].indirect(entries), prod[h][:, j0:j1], ALU.add)
             nc.sync.dma_start(out[h * P : (h + 1) * P, j0:j1], res[h][:, j0:j1])
 
         nc.vector.memset(tab_plane[:].bitcast(I32), 0)
-        nc.gpsimd.memset(warm[:], 0.0)
-        nc.scalar.activation(warm2[:], warm[:], ACT.Tanh)
+
         load_words(0)
         nc.sync.dma_start(offsets[:], offs)
         load_weight(wv_raw, wv, 0)
@@ -186,46 +171,46 @@ def tile_list_engram_hl_tanhL_kernel(
         load_words(1)
         load_weight(wk_raw, wk, 1)
         load_weight(wv_raw, wv, 1)
-        nc.sync.dma_start(st_sb[0][:], st[0:P, :])
-        nc.sync.dma_start(st_sb[1][:], st[P:N, :])
-        nc.sync.dma_start(r_sb[0][:], rT[0:P, :])
-        nc.sync.dma_start(r_sb[1][:], rT[P:N, :])
+        for h in range(HALVES):
+            nc.sync.dma_start(st_sb[h][:], st[h * P : (h + 1) * P, :])
+        for h in range(HALVES):
+            nc.sync.dma_start(r_sb[h][:], rT[h * P : (h + 1) * P, :])
 
         gather_words(0)
-        mask_hi(0, 0)
-        mask_hi(0, 1)
-        cast_hi(0, 0)
-        cast_hi(0, 1)
+        for h in range(HALVES):
+            mask_hi(0, h)
+        for h in range(HALVES):
+            cast_hi(0, h)
         cast_wk(0)
         gather_scales()
-        make_lo(0, 0)
-        make_lo(0, 1)
-        quantise(0, 0, 2)
-        quantise(0, 2, 2)
-        quantise(0, 4, 2)
+        for h in range(HALVES):
+            make_lo(0, h)
+        quantise_wk(0)
+        for h in range(HALVES):
+            quantise_wv(0, h)
         gather_words(1)
-        ke_pass(0, 0)
-        ke_pass(0, 1)
-        ve_passes(0, 0)
-        ve_passes(0, 1)
+        for h in range(HALVES):
+            ke_pass(0, h)
+        for h in range(HALVES):
+            ve_passes(0, h)
+
         cast_wk(1)
-        mask_hi(1, 0)
-        mask_hi(1, 1)
-        cast_hi(1, 0)
-        cast_hi(1, 1)
-        quantise(1, 0, 2)
-        ke_pass(1, 0)
-        ke_pass(1, 1)
-        make_lo(1, 0)
-        make_lo(1, 1)
-        quantise(1, 2, 2)
-        ve_passes(1, 0)
-        gate_of(0)
-        quantise(1, 4, 2)
-        ve_passes(1, 1)
-        gate_of(1)
-        gated(0)
-        gated(1)
-        finish(0, 0, J)
-        finish(1, 0, 384)
-        finish(1, 384, J)
+        for h in range(HALVES):
+            mask_hi(1, h)
+        for h in range(HALVES):
+            cast_hi(1, h)
+        quantise_wk(1)
+        for h in range(HALVES):
+            ke_pass(1, h)
+        for h in range(HALVES):
+            make_lo(1, h)
+        for h in range(HALVES):
+            quantise_wv(1, h)
+            ve_passes(1, h)
+            make_gate(h)
+
+        for h in range(HALVES):
+            apply_gate(h)
+        add_record_and_store(0, 0, J)
+        add_record_and_store(1, 0, LAST_CUT)
+        add_record_and_store(1, LAST_CUT, J)

@@ -22,24 +22,25 @@ HALVES = N // P
 QUADRANTS = 4
 SCALE_ROWS = 4
 PER_COLUMN = 16
-
+PARTS = 2
+PART = J // PARTS
 HI_MASK = 0xFFF00000 - (1 << 32)
-
+HI_PAIR_MASK = 0xFFF0FFF0 - (1 << 32)
 SLOTS = 6
 KEY = (0, 1)
 HI = (2, 4)
 LO = (3, 5)
 SLOT_VALUES = PACK * P
-
 LAST_CUT = 384
+RUN = 2
 
 
 def rows_walk(rows):
-    return rows.rearrange("p t (c i) -> p c t i", i=2)
+    return rows.rearrange("p t (c i) -> p c t i", i=RUN)
 
 
 def packed_walk(values):
-    return values.rearrange("p (c i t) -> p c t i", i=2, t=PACK)
+    return values.rearrange("p (c i t) -> p c t i", i=RUN, t=PACK)
 
 
 def tile_list_engram_hl_tanhL_kernel(
@@ -61,6 +62,7 @@ def tile_list_engram_hl_tanhL_kernel(
         wk_raw = tiles("wk_raw", PASSES, [P, PACK, N], F32)
         wv_raw = tiles("wv_raw", PASSES, [P, PACK, N], F32)
         wv_hi = tiles("wv_hi", PASSES, [P, PACK, N], F32)
+        wv_top = tiles("wv_top", PASSES * HALVES, [P, SLOT_VALUES], BF16)
         w_bf = tiles("w_bf", PASSES, [P, SLOTS * SLOT_VALUES], BF16)
         w_codes = tiles("w_codes", PASSES, [P, SLOTS * P], U32)
         w_plane = tiles("w_plane", PASSES, [P, SLOTS * P], U8)
@@ -70,7 +72,7 @@ def tile_list_engram_hl_tanhL_kernel(
         gate = tiles("gate", HALVES, [P, J], F32)
         prod = tiles("prod", HALVES, [P, J], F32)
         res = tiles("res", HALVES, [P, J], F32)
-        ke = [ps.tile([P, J], F32, name=f"ke{h}") for h in range(HALVES)]
+        ke = [[ps.tile([P, PART], F32, name=f"ke{h}{b}") for b in range(PARTS)] for h in range(HALVES)]
         ve = [ps.tile([P, J], F32, name=f"ve{h}") for h in range(HALVES)]
 
         def load_words(a):
@@ -93,14 +95,23 @@ def tile_list_engram_hl_tanhL_kernel(
         def half(rows, h):
             return rows[:, :, h * P : (h + 1) * P]
 
-        def gather_words(a):
-            nc.vector.tensor_copy(picked_w[a][:], tab_w[a][:].bitcast(U32).indirect(offsets[:]))
+        def entries(j0, j1):
+            return offsets[:, j0 // PER_COLUMN : j1 // PER_COLUMN]
+
+        def gather_words(a, j0=0, j1=J):
+            nc.vector.tensor_copy(picked_w[a][:, j0:j1], tab_w[a][:].bitcast(U32).indirect(entries(j0, j1)))
 
         def gather_scales():
             nc.vector.tensor_copy(picked_plane[:], tab_plane[:].indirect(offsets[:]))
 
         def cast_wk(a):
             nc.scalar.copy(packed_walk(slots(a, KEY[0], HALVES)), rows_walk(wk_raw[a][:]))
+
+        def cast_wk_half(a, h, eng="s"):
+            if eng == "s":
+                nc.scalar.copy(packed_walk(slots(a, KEY[h])), rows_walk(half(wk_raw[a], h)))
+            else:
+                nc.vector.tensor_copy(packed_walk(slots(a, KEY[h])), rows_walk(half(wk_raw[a], h)))
 
         def mask_hi(a, h):
             nc.vector.tensor_scalar(
@@ -112,102 +123,115 @@ def tile_list_engram_hl_tanhL_kernel(
 
         def make_lo(a, h):
             nc.vector.tensor_tensor(
-                packed_walk(slots(a, LO[h])),
-                rows_walk(half(wv_raw[a], h)),
-                rows_walk(half(wv_hi[a], h)),
-                ALU.subtract,
+                packed_walk(slots(a, LO[h])), rows_walk(half(wv_raw[a], h)), rows_walk(half(wv_hi[a], h)), ALU.subtract
             )
 
-        def quantise_pair(a, first):
+        def copy_top(a, h):
+            upper = half(wv_raw[a], h).bitcast(BF16).rearrange("p t (c i e) -> p c t i e", i=RUN, e=2)[:, :, :, :, 1]
+            nc.scalar.copy(packed_walk(wv_top[HALVES * a + h][:]), upper)
+
+        def mask_top(a, h):
+            nc.vector.tensor_scalar(
+                slots(a, HI[h]).bitcast(I32), wv_top[HALVES * a + h][:].bitcast(I32), HI_PAIR_MASK, None, ALU.bitwise_and
+            )
+
+        def make_lo_top(a, h):
+            nc.vector.tensor_tensor(
+                packed_walk(slots(a, LO[h])), rows_walk(half(wv_raw[a], h)), packed_walk(slots(a, HI[h])), ALU.subtract
+            )
+
+        def quantise(a, first, count):
             nc.vector.quantize_mx(
-                out=w_codes[a][:, first * P : (first + 2) * P].bitcast(FP8X4),
-                scales=w_plane[a][:, first * P : (first + 2) * P],
-                in_=slots(a, first, 2),
+                out=w_codes[a][:, first * P : (first + count) * P].bitcast(FP8X4),
+                scales=w_plane[a][:, first * P : (first + count) * P],
+                in_=slots(a, first, count),
             )
 
-        def quantise_wk(a):
-            quantise_pair(a, KEY[0])
-
-        def quantise_wv(a, h):
-            quantise_pair(a, HI[h])
-
-        def mx_pass(acc, a, slot, start, stop):
+        def mx_pass(acc, a, slot, j0, j1, start, stop):
             nc.tensor.matmul_mx(
-                out=acc[:],
+                out=acc,
                 lhsT=w_codes[a][:, slot * P : (slot + 1) * P].bitcast(FP8X4),
                 lhsT_scale=w_plane[a][:, slot * P : (slot + 1) * P],
-                rhs=picked_w[a][:].bitcast(FP8X4),
-                rhs_scale=picked_plane[SCALE_ROWS * a : P, :],
+                rhs=picked_w[a][:, j0:j1].bitcast(FP8X4),
+                rhs_scale=picked_plane[SCALE_ROWS * a : P, j0:j1],
                 start=start,
                 stop=stop,
             )
 
-        def ke_pass(a, h):
-            mx_pass(ke[h], a, KEY[h], a == 0, a == PASSES - 1)
+        def ke_pass(a, h, b):
+            mx_pass(ke[h][b][:], a, KEY[h], b * PART, (b + 1) * PART, a == 0, a == PASSES - 1)
 
         def ve_passes(a, h):
-            mx_pass(ve[h], a, HI[h], a == 0, False)
-            mx_pass(ve[h], a, LO[h], False, a == PASSES - 1)
+            mx_pass(ve[h][:], a, HI[h], 0, J, a == 0, False)
+            mx_pass(ve[h][:], a, LO[h], 0, J, False, a == PASSES - 1)
 
-        def make_gate(h):
-            nc.vector.tensor_tensor(z[h][:], ke[h][:], st_sb[h][:], ALU.mult)
-            nc.scalar.activation(gate[h][:], z[h][:], ACT.Tanh)
+        def make_gate(h, b):
+            cols = slice(b * PART, (b + 1) * PART)
+            nc.vector.tensor_tensor(z[h][:, cols], ke[h][b][:], st_sb[h][:, cols], ALU.mult)
+            nc.scalar.activation(gate[h][:, cols], z[h][:, cols], ACT.Tanh)
 
         def apply_gate(h):
             nc.vector.tensor_tensor(prod[h][:], ve[h][:], gate[h][:], ALU.mult)
 
         def add_record_and_store(h, j0, j1):
-            entries = offsets[:, j0 // PER_COLUMN : j1 // PER_COLUMN]
-            nc.vector.tensor_tensor(res[h][:, j0:j1], r_sb[h][:].indirect(entries), prod[h][:, j0:j1], ALU.add)
+            nc.vector.tensor_tensor(res[h][:, j0:j1], r_sb[h][:].indirect(entries(j0, j1)), prod[h][:, j0:j1], ALU.add)
             nc.sync.dma_start(out[h * P : (h + 1) * P, j0:j1], res[h][:, j0:j1])
 
         nc.vector.memset(tab_plane[:].bitcast(I32), 0)
 
         load_words(0)
         nc.sync.dma_start(offsets[:], offs)
-        load_weight(wv_raw, wv, 0)
         load_scales()
-        load_weight(wk_raw, wk, 0)
-        load_words(1)
-        load_weight(wk_raw, wk, 1)
+        load_weight(wv_raw, wv, 0)
         load_weight(wv_raw, wv, 1)
-        for h in range(HALVES):
-            nc.sync.dma_start(st_sb[h][:], st[h * P : (h + 1) * P, :])
-        for h in range(HALVES):
-            nc.sync.dma_start(r_sb[h][:], rT[h * P : (h + 1) * P, :])
+        load_weight(wk_raw, wk, 0)
+        load_weight(wk_raw, wk, 1)
+        load_words(1)
+        nc.sync.dma_start(st_sb[0][:], st[0:P, :])
+        nc.sync.dma_start(st_sb[1][:], st[P : 2 * P, :])
+        nc.sync.dma_start(r_sb[0][:], rT[0:P, :])
+        nc.sync.dma_start(r_sb[1][:], rT[P : 2 * P, :])
 
         gather_words(0)
-        for h in range(HALVES):
-            mask_hi(0, h)
-        for h in range(HALVES):
-            cast_hi(0, h)
-        cast_wk(0)
         gather_scales()
         for h in range(HALVES):
-            make_lo(0, h)
-        quantise_wk(0)
+            copy_top(0, h)
         for h in range(HALVES):
-            quantise_wv(0, h)
-        gather_words(1)
-        for h in range(HALVES):
-            ke_pass(0, h)
-        for h in range(HALVES):
-            ve_passes(0, h)
-
+            copy_top(1, h)
+        cast_wk(0)
         cast_wk(1)
         for h in range(HALVES):
-            mask_hi(1, h)
+            mask_top(0, h)
         for h in range(HALVES):
-            cast_hi(1, h)
-        quantise_wk(1)
+            make_lo_top(0, h)
         for h in range(HALVES):
-            ke_pass(1, h)
+            quantise(0, HI[h], 2)
         for h in range(HALVES):
-            make_lo(1, h)
+            ve_passes(0, h)
         for h in range(HALVES):
-            quantise_wv(1, h)
+            mask_top(1, h)
+        for h in range(HALVES):
+            make_lo_top(1, h)
+        for h in range(HALVES):
+            quantise(1, HI[h], 2)
+        quantise(0, KEY[0], 2)
+        for h in range(HALVES):
+            ke_pass(0, h, 0)
+        for h in range(HALVES):
+            ke_pass(0, h, 1)
+        quantise(1, KEY[0], 2)
+        gather_words(1, 0, PART)
+        gather_words(1, PART, J)
+        for h in range(HALVES):
+            ke_pass(1, h, 0)
+        for h in range(HALVES):
+            ke_pass(1, h, 1)
+        for h in range(HALVES):
             ve_passes(1, h)
-            make_gate(h)
+        for h in range(HALVES):
+            make_gate(0, h)
+        for h in range(HALVES):
+            make_gate(1, h)
 
         for h in range(HALVES):
             apply_gate(h)

@@ -170,8 +170,8 @@ def tile_list_engram_hl_tanhL_kernel(
             nc.vector.tensor_tensor(z[h][:, cols], ke[h][b][:], st_sb[h][:, cols], ALU.mult)
             nc.scalar.activation(gate[h][:, cols], z[h][:, cols], ACT.Tanh)
 
-        def apply_gate(h):
-            nc.vector.tensor_tensor(prod[h][:], ve[h][:], gate[h][:], ALU.mult)
+        def apply_gate(h, j0=0, j1=J):
+            nc.vector.tensor_tensor(prod[h][:, j0:j1], ve[h][:, j0:j1], gate[h][:, j0:j1], ALU.mult)
 
         def add_record_and_store(h, j0, j1):
             nc.vector.tensor_tensor(res[h][:, j0:j1], r_sb[h][:].indirect(entries(j0, j1)), prod[h][:, j0:j1], ALU.add)
@@ -200,21 +200,21 @@ def tile_list_engram_hl_tanhL_kernel(
             copy_top(1, h)
         cast_wk(0)
         cast_wk(1)
-        for h in range(HALVES):
-            mask_top(0, h)
-        for h in range(HALVES):
-            make_lo_top(0, h)
-        for h in range(HALVES):
-            quantise(0, HI[h], 2)
+        mask_top(0, 0)
+        make_lo_top(0, 0)
+        mask_top(0, 1)
+        quantise(0, HI[0], 2)
+        make_lo_top(0, 1)
+        mask_top(1, 0)
+        quantise(0, HI[1], 2)
         for h in range(HALVES):
             ve_passes(0, h)
-        for h in range(HALVES):
-            mask_top(1, h)
-        for h in range(HALVES):
-            make_lo_top(1, h)
-        for h in range(HALVES):
-            quantise(1, HI[h], 2)
+        make_lo_top(1, 0)
+        mask_top(1, 1)
+        quantise(1, HI[0], 2)
+        make_lo_top(1, 1)
         quantise(0, KEY[0], 2)
+        quantise(1, HI[1], 2)
         for h in range(HALVES):
             ke_pass(0, h, 0)
         for h in range(HALVES):
@@ -229,12 +229,13 @@ def tile_list_engram_hl_tanhL_kernel(
         for h in range(HALVES):
             ve_passes(1, h)
         for h in range(HALVES):
-            make_gate(0, h)
+            make_gate(h, 0)
         for h in range(HALVES):
-            make_gate(1, h)
-
-        for h in range(HALVES):
-            apply_gate(h)
-        add_record_and_store(0, 0, J)
+            make_gate(h, 1)
+        apply_gate(0, 0, PART)
+        apply_gate(0, PART, J)
+        add_record_and_store(0, 0, PART)
+        apply_gate(1)
+        add_record_and_store(0, PART, J)
         add_record_and_store(1, 0, LAST_CUT)
         add_record_and_store(1, LAST_CUT, J)

@@ -219,8 +219,8 @@ def tile_list_engram_hl_tanhL_kernel(
             ke_pass(0, h, 0)
         for h in range(HALVES):
             ke_pass(0, h, 1)
-        quantise(1, KEY[0], 2)
         gather_words(1, 0, PART)
+        quantise(1, KEY[0], 2)
         gather_words(1, PART, J)
         for h in range(HALVES):
             ke_pass(1, h, 0)

@@ -58,18 +58,18 @@ def tile_list_engram_hl_tanhL_kernel(
         tab_plane = sb.tile([P, T], U8, name="tab_plane", align_bytes=64)
         picked_plane = sb.tile([P, J], U8, name="picked_plane", align_bytes=64)
         tab_w = tiles("tab_w", PASSES, [P, T], I32)
-        picked_w = tiles("picked_w", PASSES, [P, J], U32)
-        wk_raw = tiles("wk_raw", PASSES, [P, PACK, N], F32)
+        picked_w = {}
+        wk_raw = [sb.tile([P, PACK, N], F32, name=f"wk_raw{a}", tag=f"wk_raw{a}", align_bytes=64) for a in range(PASSES)]
         wv_raw = tiles("wv_raw", PASSES, [P, PACK, N], F32)
         wv_hi = tiles("wv_hi", PASSES, [P, PACK, N], F32)
         wv_top = tiles("wv_top", PASSES * HALVES, [P, SLOT_VALUES], BF16)
-        w_bf = tiles("w_bf", PASSES, [P, SLOTS * SLOT_VALUES], BF16)
-        w_codes = tiles("w_codes", PASSES, [P, SLOTS * P], U32)
+        pairs = {}
+        codes = {}
         w_plane = tiles("w_plane", PASSES, [P, SLOTS * P], U8)
         st_sb = tiles("st_sb", HALVES, [P, J], F32)
         r_sb = tiles("r_sb", HALVES, [P, T], F32)
         z = tiles("z", HALVES, [P, J], F32)
-        gate = tiles("gate", HALVES, [P, J], F32)
+        gate = [[sb.tile([P, PART], F32, name=f"gate{h}{b}", tag=f"gate{h}{b}", align_bytes=64) for b in range(PARTS)] for h in range(HALVES)]
         prod = tiles("prod", HALVES, [P, J], F32)
         res = tiles("res", HALVES, [P, J], F32)
         ke = [[ps.tile([P, PART], F32, name=f"ke{h}{b}") for b in range(PARTS)] for h in range(HALVES)]
@@ -89,8 +89,22 @@ def tile_list_engram_hl_tanhL_kernel(
                     tab_scales[:, SCALE_ROWS * quad : SCALE_ROWS * (quad + 1), :].bitcast(I32),
                 )
 
+        def open_pair(a, first, tag):
+            pairs[(a, first)] = sb.tile([P, 2 * SLOT_VALUES], BF16, name=f"bf{a}{first}", tag=tag, align_bytes=64)
+
+        def open_codes(a, first, tag):
+            codes[(a, first)] = sb.tile([P, 2 * P], U32, name=f"codes{a}{first}", tag=tag, align_bytes=64)
+
+        def slot_codes(a, first, count=1):
+            at = first % 2
+            return codes[(a, first - at)][:, at * P : (at + count) * P].bitcast(FP8X4)
+
+        def open_picked(a, tag):
+            picked_w[a] = sb.tile([P, J], U32, name=f"picked_w{a}", tag=tag, align_bytes=64)
+
         def slots(a, first, count=1):
-            return w_bf[a][:, first * SLOT_VALUES : (first + count) * SLOT_VALUES]
+            at = first % 2
+            return pairs[(a, first - at)][:, at * SLOT_VALUES : (at + count) * SLOT_VALUES]
 
         def half(rows, h):
             return rows[:, :, h * P : (h + 1) * P]
@@ -140,9 +154,17 @@ def tile_list_engram_hl_tanhL_kernel(
                 packed_walk(slots(a, LO[h])), rows_walk(half(wv_raw[a], h)), packed_walk(slots(a, HI[h])), ALU.subtract
             )
 
+        def make_lo_pool(a, h):
+            nc.gpsimd.tensor_tensor(
+                slots(a, LO[h]).rearrange("p (n t) -> p n t", t=PACK),
+                half(wv_raw[a], h).rearrange("p t n -> p n t"),
+                slots(a, HI[h]).rearrange("p (n t) -> p n t", t=PACK),
+                ALU.subtract,
+            )
+
         def quantise(a, first, count):
             nc.vector.quantize_mx(
-                out=w_codes[a][:, first * P : (first + count) * P].bitcast(FP8X4),
+                out=slot_codes(a, first, count),
                 scales=w_plane[a][:, first * P : (first + count) * P],
                 in_=slots(a, first, count),
             )
@@ -150,7 +172,7 @@ def tile_list_engram_hl_tanhL_kernel(
         def mx_pass(acc, a, slot, j0, j1, start, stop):
             nc.tensor.matmul_mx(
                 out=acc,
-                lhsT=w_codes[a][:, slot * P : (slot + 1) * P].bitcast(FP8X4),
+                lhsT=slot_codes(a, slot),
                 lhsT_scale=w_plane[a][:, slot * P : (slot + 1) * P],
                 rhs=picked_w[a][:, j0:j1].bitcast(FP8X4),
                 rhs_scale=picked_plane[SCALE_ROWS * a : P, j0:j1],
@@ -168,10 +190,11 @@ def tile_list_engram_hl_tanhL_kernel(
         def make_gate(h, b):
             cols = slice(b * PART, (b + 1) * PART)
             nc.vector.tensor_tensor(z[h][:, cols], ke[h][b][:], st_sb[h][:, cols], ALU.mult)
-            nc.scalar.activation(gate[h][:, cols], z[h][:, cols], ACT.Tanh)
+            nc.scalar.activation(gate[h][b][:], z[h][:, cols], ACT.Tanh)
 
-        def apply_gate(h, j0=0, j1=J):
-            nc.vector.tensor_tensor(prod[h][:, j0:j1], ve[h][:, j0:j1], gate[h][:, j0:j1], ALU.mult)
+        def apply_gate(h, b):
+            cols = slice(b * PART, (b + 1) * PART)
+            nc.vector.tensor_tensor(prod[h][:, cols], ve[h][:, cols], gate[h][b][:], ALU.mult)
 
         def add_record_and_store(h, j0, j1):
             nc.vector.tensor_tensor(res[h][:, j0:j1], r_sb[h][:].indirect(entries(j0, j1)), prod[h][:, j0:j1], ALU.add)
@@ -192,6 +215,17 @@ def tile_list_engram_hl_tanhL_kernel(
         nc.sync.dma_start(r_sb[0][:], rT[0:P, :])
         nc.sync.dma_start(r_sb[1][:], rT[P : 2 * P, :])
 
+        open_picked(0, "pw0")
+        open_codes(0, 0, "c00")
+        open_codes(0, 2, "c02")
+        open_codes(0, 4, "c04")
+        open_codes(1, 0, "c10")
+        open_codes(1, 2, "c12")
+        open_pair(0, 0, "k0")
+        open_pair(1, 0, "k1")
+        open_pair(0, 2, "v00")
+        open_pair(0, 4, "v01")
+        open_pair(1, 2, "v10")
         gather_words(0)
         gather_scales()
         for h in range(HALVES):
@@ -200,6 +234,7 @@ def tile_list_engram_hl_tanhL_kernel(
             copy_top(1, h)
         cast_wk(0)
         cast_wk(1)
+        open_picked(1, "wk_raw1")
         mask_top(0, 0)
         make_lo_top(0, 0)
         mask_top(0, 1)
@@ -210,11 +245,8 @@ def tile_list_engram_hl_tanhL_kernel(
         for h in range(HALVES):
             ve_passes(0, h)
         make_lo_top(1, 0)
-        mask_top(1, 1)
-        quantise(1, HI[0], 2)
-        make_lo_top(1, 1)
         quantise(0, KEY[0], 2)
-        quantise(1, HI[1], 2)
+        quantise(1, HI[0], 2)
         for h in range(HALVES):
             ke_pass(0, h, 0)
         for h in range(HALVES):
@@ -222,20 +254,26 @@ def tile_list_engram_hl_tanhL_kernel(
         gather_words(1, 0, PART)
         quantise(1, KEY[0], 2)
         gather_words(1, PART, J)
+        open_pair(1, 4, "k1")
+        mask_top(1, 1)
+        make_lo_pool(1, 1)
         for h in range(HALVES):
             ke_pass(1, h, 0)
         for h in range(HALVES):
             ke_pass(1, h, 1)
-        for h in range(HALVES):
-            ve_passes(1, h)
+        ve_passes(1, 0)
         for h in range(HALVES):
             make_gate(h, 0)
         for h in range(HALVES):
             make_gate(h, 1)
-        apply_gate(0, 0, PART)
-        apply_gate(0, PART, J)
-        add_record_and_store(0, 0, PART)
-        apply_gate(1)
-        add_record_and_store(0, PART, J)
+        apply_gate(0, 0)
+        apply_gate(0, 1)
+        open_codes(1, 4, "gate00")
+        quantise(1, HI[1], 2)
+        ve_passes(1, 1)
+        add_record_and_store(0, 0, LAST_CUT)
+        apply_gate(1, 0)
+        apply_gate(1, 1)
+        add_record_and_store(0, LAST_CUT, J)
         add_record_and_store(1, 0, LAST_CUT)
         add_record_and_store(1, LAST_CUT, J)

@@ -58,11 +58,12 @@ def tile_list_engram_hl_tanhL_kernel(
         tab_plane = sb.tile([P, T], U8, name="tab_plane", align_bytes=64)
         picked_plane = sb.tile([P, J], U8, name="picked_plane", align_bytes=64)
         tab_w = tiles("tab_w", PASSES, [P, T], I32)
-        picked_w = {}
+        picked_first = sb.tile([P, J], U32, name="picked_first", align_bytes=64)
+        picked = {(0, b): picked_first[:, b * PART : (b + 1) * PART] for b in range(PARTS)}
         wk_raw = [sb.tile([P, PACK, N], F32, name=f"wk_raw{a}", tag=f"wk_raw{a}", align_bytes=64) for a in range(PASSES)]
         wv_raw = tiles("wv_raw", PASSES, [P, PACK, N], F32)
         wv_hi = tiles("wv_hi", PASSES, [P, PACK, N], F32)
-        wv_top = tiles("wv_top", PASSES * HALVES, [P, SLOT_VALUES], BF16)
+        wv_top = {}
         pairs = {}
         codes = {}
         w_plane = tiles("w_plane", PASSES, [P, SLOTS * P], U8)
@@ -73,7 +74,11 @@ def tile_list_engram_hl_tanhL_kernel(
         prod = tiles("prod", HALVES, [P, J], F32)
         res = tiles("res", HALVES, [P, J], F32)
         ke = [[ps.tile([P, PART], F32, name=f"ke{h}{b}") for b in range(PARTS)] for h in range(HALVES)]
-        ve = [ps.tile([P, J], F32, name=f"ve{h}") for h in range(HALVES)]
+        ve_whole = ps.tile([P, J], F32, name="ve0")
+        ve = [
+            [ve_whole[:, b * PART : (b + 1) * PART] for b in range(PARTS)],
+            [ps.tile([P, PART], F32, name=f"ve1{b}")[:] for b in range(PARTS)],
+        ]
 
         def load_words(a):
             nc.sync.dma_start(tab_w[a][:], tab_words[a].rearrange("p t i -> p (t i)").bitcast(I32))
@@ -99,8 +104,11 @@ def tile_list_engram_hl_tanhL_kernel(
             at = first % 2
             return codes[(a, first - at)][:, at * P : (at + count) * P].bitcast(FP8X4)
 
-        def open_picked(a, tag):
-            picked_w[a] = sb.tile([P, J], U32, name=f"picked_w{a}", tag=tag, align_bytes=64)
+        def open_picked(b, tag):
+            picked[(1, b)] = sb.tile([P, PART], U32, name=f"picked1{b}", tag=tag, align_bytes=64)[:]
+
+        def open_top(a, h, tag):
+            wv_top[HALVES * a + h] = sb.tile([P, SLOT_VALUES], BF16, name=f"top{a}{h}", tag=tag, align_bytes=64)
 
         def slots(a, first, count=1):
             at = first % 2
@@ -112,8 +120,11 @@ def tile_list_engram_hl_tanhL_kernel(
         def entries(j0, j1):
             return offsets[:, j0 // PER_COLUMN : j1 // PER_COLUMN]
 
-        def gather_words(a, j0=0, j1=J):
-            nc.vector.tensor_copy(picked_w[a][:, j0:j1], tab_w[a][:].bitcast(U32).indirect(entries(j0, j1)))
+        def gather_first():
+            nc.vector.tensor_copy(picked_first[:], tab_w[0][:].bitcast(U32).indirect(offsets[:]))
+
+        def gather_words(b):
+            nc.vector.tensor_copy(picked[(1, b)], tab_w[1][:].bitcast(U32).indirect(entries(b * PART, (b + 1) * PART)))
 
         def gather_scales():
             nc.vector.tensor_copy(picked_plane[:], tab_plane[:].indirect(offsets[:]))
@@ -169,32 +180,37 @@ def tile_list_engram_hl_tanhL_kernel(
                 in_=slots(a, first, count),
             )
 
-        def mx_pass(acc, a, slot, j0, j1, start, stop):
+        def mx_pass(acc, a, slot, words, j0, j1, start, stop):
             nc.tensor.matmul_mx(
                 out=acc,
                 lhsT=slot_codes(a, slot),
                 lhsT_scale=w_plane[a][:, slot * P : (slot + 1) * P],
-                rhs=picked_w[a][:, j0:j1].bitcast(FP8X4),
+                rhs=words.bitcast(FP8X4),
                 rhs_scale=picked_plane[SCALE_ROWS * a : P, j0:j1],
                 start=start,
                 stop=stop,
             )
 
         def ke_pass(a, h, b):
-            mx_pass(ke[h][b][:], a, KEY[h], b * PART, (b + 1) * PART, a == 0, a == PASSES - 1)
+            mx_pass(ke[h][b][:], a, KEY[h], picked[(a, b)], b * PART, (b + 1) * PART, a == 0, a == PASSES - 1)
 
-        def ve_passes(a, h):
-            mx_pass(ve[h][:], a, HI[h], 0, J, a == 0, False)
-            mx_pass(ve[h][:], a, LO[h], 0, J, False, a == PASSES - 1)
+        def ve_whole_first():
+            mx_pass(ve_whole[:], 0, HI[0], picked_first[:], 0, J, True, False)
+            mx_pass(ve_whole[:], 0, LO[0], picked_first[:], 0, J, False, False)
+
+        def ve_part(a, h, b):
+            j0, j1 = b * PART, (b + 1) * PART
+            mx_pass(ve[h][b], a, HI[h], picked[(a, b)], j0, j1, a == 0, False)
+            mx_pass(ve[h][b], a, LO[h], picked[(a, b)], j0, j1, False, a == PASSES - 1 and (h == 1 or b == PARTS - 1))
 
         def make_gate(h, b):
             cols = slice(b * PART, (b + 1) * PART)
-            nc.vector.tensor_tensor(z[h][:, cols], ke[h][b][:], st_sb[h][:, cols], ALU.mult)
+            nc.vector.tensor_tensor(z[h][:, cols], st_sb[h][:, cols], ke[h][b][:], ALU.mult)
             nc.scalar.activation(gate[h][b][:], z[h][:, cols], ACT.Tanh)
 
         def apply_gate(h, b):
             cols = slice(b * PART, (b + 1) * PART)
-            nc.vector.tensor_tensor(prod[h][:, cols], ve[h][:, cols], gate[h][b][:], ALU.mult)
+            nc.vector.tensor_tensor(prod[h][:, cols], gate[h][b][:], ve[h][b], ALU.mult)
 
         def add_record_and_store(h, j0, j1):
             nc.vector.tensor_tensor(res[h][:, j0:j1], r_sb[h][:].indirect(entries(j0, j1)), prod[h][:, j0:j1], ALU.add)
@@ -215,7 +231,6 @@ def tile_list_engram_hl_tanhL_kernel(
         nc.sync.dma_start(r_sb[0][:], rT[0:P, :])
         nc.sync.dma_start(r_sb[1][:], rT[P : 2 * P, :])
 
-        open_picked(0, "pw0")
         open_codes(0, 0, "c00")
         open_codes(0, 2, "c02")
         open_codes(0, 4, "c04")
@@ -226,14 +241,19 @@ def tile_list_engram_hl_tanhL_kernel(
         open_pair(0, 2, "v00")
         open_pair(0, 4, "v01")
         open_pair(1, 2, "v10")
-        gather_words(0)
+        open_top(0, 0, "t00")
+        open_top(0, 1, "t01")
+        open_top(1, 0, "t10")
+        open_picked(0, "p10")
+        gather_first()
         gather_scales()
         for h in range(HALVES):
             copy_top(0, h)
-        for h in range(HALVES):
-            copy_top(1, h)
+        copy_top(1, 0)
         cast_wk(0)
         cast_wk(1)
+        open_top(1, 1, "wk_raw0")
+        copy_top(1, 1)
         open_picked(1, "wk_raw1")
         mask_top(0, 0)
         make_lo_top(0, 0)
@@ -242,8 +262,9 @@ def tile_list_engram_hl_tanhL_kernel(
         make_lo_top(0, 1)
         mask_top(1, 0)
         quantise(0, HI[1], 2)
+        ve_whole_first()
         for h in range(HALVES):
-            ve_passes(0, h)
+            ve_part(0, 1, h)
         make_lo_top(1, 0)
         quantise(0, KEY[0], 2)
         quantise(1, HI[0], 2)
@@ -251,9 +272,9 @@ def tile_list_engram_hl_tanhL_kernel(
             ke_pass(0, h, 0)
         for h in range(HALVES):
             ke_pass(0, h, 1)
-        gather_words(1, 0, PART)
+        gather_words(0)
         quantise(1, KEY[0], 2)
-        gather_words(1, PART, J)
+        gather_words(1)
         open_pair(1, 4, "k1")
         mask_top(1, 1)
         make_lo_pool(1, 1)
@@ -261,7 +282,8 @@ def tile_list_engram_hl_tanhL_kernel(
             ke_pass(1, h, 0)
         for h in range(HALVES):
             ke_pass(1, h, 1)
-        ve_passes(1, 0)
+        for h in range(HALVES):
+            ve_part(1, 0, h)
         for h in range(HALVES):
             make_gate(h, 0)
         for h in range(HALVES):
@@ -270,10 +292,12 @@ def tile_list_engram_hl_tanhL_kernel(
         apply_gate(0, 1)
         open_codes(1, 4, "gate00")
         quantise(1, HI[1], 2)
-        ve_passes(1, 1)
+        for h in range(HALVES):
+            ve_part(1, 1, h)
         add_record_and_store(0, 0, LAST_CUT)
         apply_gate(1, 0)
-        apply_gate(1, 1)
         add_record_and_store(0, LAST_CUT, J)
-        add_record_and_store(1, 0, LAST_CUT)
+        apply_gate(1, 1)
+        add_record_and_store(1, 0, PART)
+        add_record_and_store(1, PART, LAST_CUT)
         add_record_and_store(1, LAST_CUT, J)

@@ -65,6 +65,8 @@ def tile_list_engram_hl_tanhL_kernel(
         wv_hi = tiles("wv_hi", PASSES, [P, PACK, N], F32)
         wv_top = {}
         pairs = {}
+        singles = {}
+        single_codes = {}
         codes = {}
         w_plane = tiles("w_plane", PASSES, [P, SLOTS * P], U8)
         st_sb = tiles("st_sb", HALVES, [P, J], F32)
@@ -100,7 +102,12 @@ def tile_list_engram_hl_tanhL_kernel(
         def open_codes(a, first, tag):
             codes[(a, first)] = sb.tile([P, 2 * P], U32, name=f"codes{a}{first}", tag=tag, align_bytes=64)
 
+        def open_single_codes(key, tag):
+            single_codes[key] = sb.tile([P, P], U32, name=f"single_codes{key[1]}", tag=tag, align_bytes=64)
+
         def slot_codes(a, first, count=1):
+            if (a, first) in single_codes:
+                return single_codes[(a, first)][:].bitcast(FP8X4)
             at = first % 2
             return codes[(a, first - at)][:, at * P : (at + count) * P].bitcast(FP8X4)
 
@@ -110,7 +117,12 @@ def tile_list_engram_hl_tanhL_kernel(
         def open_top(a, h, tag):
             wv_top[HALVES * a + h] = sb.tile([P, SLOT_VALUES], BF16, name=f"top{a}{h}", tag=tag, align_bytes=64)
 
+        def open_single(key, tag):
+            singles[key] = sb.tile([P, SLOT_VALUES], BF16, name=f"single{key[1]}", tag=tag, align_bytes=64)
+
         def slots(a, first, count=1):
+            if (a, first) in singles:
+                return singles[(a, first)][:]
             at = first % 2
             return pairs[(a, first - at)][:, at * SLOT_VALUES : (at + count) * SLOT_VALUES]
 
@@ -236,24 +248,26 @@ def tile_list_engram_hl_tanhL_kernel(
         open_codes(0, 4, "c04")
         open_codes(1, 0, "c10")
         open_codes(1, 2, "c12")
+        open_single_codes((1, 4), "c14")
         open_pair(0, 0, "k0")
         open_pair(1, 0, "k1")
         open_pair(0, 2, "v00")
         open_pair(0, 4, "v01")
         open_pair(1, 2, "v10")
+        open_single((1, 4), "hi11")
         open_top(0, 0, "t00")
         open_top(0, 1, "t01")
         open_top(1, 0, "t10")
+        open_top(1, 1, "t11")
         open_picked(0, "p10")
         gather_first()
         gather_scales()
         for h in range(HALVES):
             copy_top(0, h)
-        copy_top(1, 0)
+        for h in range(HALVES):
+            copy_top(1, h)
         cast_wk(0)
         cast_wk(1)
-        open_top(1, 1, "wk_raw0")
-        copy_top(1, 1)
         open_picked(1, "wk_raw1")
         mask_top(0, 0)
         make_lo_top(0, 0)
@@ -266,8 +280,10 @@ def tile_list_engram_hl_tanhL_kernel(
         for h in range(HALVES):
             ve_part(0, 1, h)
         make_lo_top(1, 0)
-        quantise(0, KEY[0], 2)
+        mask_top(1, 1)
         quantise(1, HI[0], 2)
+        quantise(1, HI[1], 1)
+        quantise(0, KEY[0], 2)
         for h in range(HALVES):
             ke_pass(0, h, 0)
         for h in range(HALVES):
@@ -275,8 +291,7 @@ def tile_list_engram_hl_tanhL_kernel(
         gather_words(0)
         quantise(1, KEY[0], 2)
         gather_words(1)
-        open_pair(1, 4, "k1")
-        mask_top(1, 1)
+        open_single((1, 5), "k1")
         make_lo_pool(1, 1)
         for h in range(HALVES):
             ke_pass(1, h, 0)
@@ -290,8 +305,8 @@ def tile_list_engram_hl_tanhL_kernel(
             make_gate(h, 1)
         apply_gate(0, 0)
         apply_gate(0, 1)
-        open_codes(1, 4, "gate00")
-        quantise(1, HI[1], 2)
+        open_single_codes((1, 5), "gate00")
+        quantise(1, LO[1], 1)
         for h in range(HALVES):
             ve_part(1, 1, h)
         add_record_and_store(0, 0, LAST_CUT)

@@ -59,7 +59,10 @@ def tile_list_engram_hl_tanhL_kernel(
         picked_plane = sb.tile([P, J], U8, name="picked_plane", align_bytes=64)
         tab_w = tiles("tab_w", PASSES, [P, T], I32)
         picked_first = sb.tile([P, J], U32, name="picked_first", align_bytes=64)
-        picked = {(0, b): picked_first[:, b * PART : (b + 1) * PART] for b in range(PARTS)}
+        picked_last = sb.tile([P, J], U32, name="picked_last", align_bytes=64)
+        picked_whole = [picked_first, picked_last]
+        picked = {(a, b): picked_whole[a][:, b * PART : (b + 1) * PART] for a in range(PASSES) for b in range(PARTS)}
+        gate_whole = sb.tile([P, J], F32, name="gate_whole", align_bytes=64)
         wk_raw = [sb.tile([P, PACK, N], F32, name=f"wk_raw{a}", tag=f"wk_raw{a}", align_bytes=64) for a in range(PASSES)]
         wv_raw = tiles("wv_raw", PASSES, [P, PACK, N], F32)
         wv_hi = tiles("wv_hi", PASSES, [P, PACK, N], F32)
@@ -72,10 +75,11 @@ def tile_list_engram_hl_tanhL_kernel(
         st_sb = tiles("st_sb", HALVES, [P, J], F32)
         r_sb = tiles("r_sb", HALVES, [P, T], F32)
         z = tiles("z", HALVES, [P, J], F32)
-        gate = [[sb.tile([P, PART], F32, name=f"gate{h}{b}", tag=f"gate{h}{b}", align_bytes=64) for b in range(PARTS)] for h in range(HALVES)]
+        gate = [[sb.tile([P, PART], F32, name=f"gate{h}{b}", tag=f"gate{h}{b}", align_bytes=64) for b in range(PARTS)] for h in range(1)]
         prod = tiles("prod", HALVES, [P, J], F32)
         res = tiles("res", HALVES, [P, J], F32)
-        ke = [[ps.tile([P, PART], F32, name=f"ke{h}{b}") for b in range(PARTS)] for h in range(HALVES)]
+        ke = [[ps.tile([P, PART], F32, name=f"ke0{b}") for b in range(PARTS)]]
+        ke_whole = ps.tile([P, J], F32, name="ke1")
         ve_whole = ps.tile([P, J], F32, name="ve0")
         ve = [
             [ve_whole[:, b * PART : (b + 1) * PART] for b in range(PARTS)],
@@ -185,10 +189,15 @@ def tile_list_engram_hl_tanhL_kernel(
                 ALU.subtract,
             )
 
+        def plane(a, first, count=1):
+            if (a, first) == (1, KEY[1]):
+                return w_plane[a][SCALE_ROWS:P, HI[0] * P : (HI[0] + 1) * P]
+            return w_plane[a][:, first * P : (first + count) * P]
+
         def quantise(a, first, count):
             nc.vector.quantize_mx(
                 out=slot_codes(a, first, count),
-                scales=w_plane[a][:, first * P : (first + count) * P],
+                scales=plane(a, first, count),
                 in_=slots(a, first, count),
             )
 
@@ -196,7 +205,7 @@ def tile_list_engram_hl_tanhL_kernel(
             nc.tensor.matmul_mx(
                 out=acc,
                 lhsT=slot_codes(a, slot),
-                lhsT_scale=w_plane[a][:, slot * P : (slot + 1) * P],
+                lhsT_scale=plane(a, slot),
                 rhs=words.bitcast(FP8X4),
                 rhs_scale=picked_plane[SCALE_ROWS * a : P, j0:j1],
                 start=start,
@@ -209,6 +218,26 @@ def tile_list_engram_hl_tanhL_kernel(
         def ve_whole_first():
             mx_pass(ve_whole[:], 0, HI[0], picked_first[:], 0, J, True, False)
             mx_pass(ve_whole[:], 0, LO[0], picked_first[:], 0, J, False, False)
+
+        def ve_late(b):
+            j0, j1 = b * PART, (b + 1) * PART
+            mx_pass(ve[1][b], 1, LO[1], picked[(1, b)], j0, j1, False, False)
+            mx_pass(ve[1][b], 1, HI[1], picked[(1, b)], j0, j1, False, True)
+
+        def ke_whole_pass(a):
+            mx_pass(ke_whole[:], a, KEY[1], picked_whole[a][:], 0, J, a == 0, a == PASSES - 1)
+
+        def ve_whole_last():
+            mx_pass(ve_whole[:], 1, HI[0], picked_last[:], 0, J, False, False)
+            mx_pass(ve_whole[:], 1, LO[0], picked_last[:], 0, J, False, True)
+
+        def make_gate_whole():
+            nc.vector.tensor_tensor(z[1][:], st_sb[1][:], ke_whole[:], ALU.mult)
+            nc.scalar.activation(gate_whole[:], z[1][:], ACT.Tanh)
+
+        def apply_gate_late(b):
+            cols = slice(b * PART, (b + 1) * PART)
+            nc.vector.tensor_tensor(prod[1][:, cols], gate_whole[:, cols], ve[1][b], ALU.mult)
 
         def ve_part(a, h, b):
             j0, j1 = b * PART, (b + 1) * PART
@@ -250,7 +279,8 @@ def tile_list_engram_hl_tanhL_kernel(
         open_codes(1, 2, "c12")
         open_single_codes((1, 4), "c14")
         open_pair(0, 0, "k0")
-        open_pair(1, 0, "k1")
+        open_single((1, 0), "k10")
+        open_single((1, 1), "k11")
         open_pair(0, 2, "v00")
         open_pair(0, 4, "v01")
         open_pair(1, 2, "v10")
@@ -259,7 +289,6 @@ def tile_list_engram_hl_tanhL_kernel(
         open_top(0, 1, "t01")
         open_top(1, 0, "t10")
         open_top(1, 1, "t11")
-        open_picked(0, "p10")
         gather_first()
         gather_scales()
         for h in range(HALVES):
@@ -267,8 +296,8 @@ def tile_list_engram_hl_tanhL_kernel(
         for h in range(HALVES):
             copy_top(1, h)
         cast_wk(0)
-        cast_wk(1)
-        open_picked(1, "wk_raw1")
+        for h in range(HALVES):
+            cast_wk_half(1, h)
         mask_top(0, 0)
         make_lo_top(0, 0)
         mask_top(0, 1)
@@ -285,34 +314,31 @@ def tile_list_engram_hl_tanhL_kernel(
         quantise(1, HI[1], 1)
         quantise(0, KEY[0], 2)
         for h in range(HALVES):
-            ke_pass(0, h, 0)
-        for h in range(HALVES):
-            ke_pass(0, h, 1)
+            ke_pass(0, 0, h)
+        ke_whole_pass(0)
         gather_words(0)
-        quantise(1, KEY[0], 2)
+        quantise(1, KEY[0], 1)
         gather_words(1)
-        open_single((1, 5), "k1")
+        quantise(1, KEY[1], 1)
+        open_single((1, 5), "k11")
         make_lo_pool(1, 1)
         for h in range(HALVES):
-            ke_pass(1, h, 0)
+            ke_pass(1, 0, h)
+        ke_whole_pass(1)
+        ve_whole_last()
         for h in range(HALVES):
-            ke_pass(1, h, 1)
-        for h in range(HALVES):
-            ve_part(1, 0, h)
-        for h in range(HALVES):
-            make_gate(h, 0)
-        for h in range(HALVES):
-            make_gate(h, 1)
+            make_gate(0, h)
+        make_gate_whole()
         apply_gate(0, 0)
         apply_gate(0, 1)
         open_single_codes((1, 5), "gate00")
         quantise(1, LO[1], 1)
         for h in range(HALVES):
-            ve_part(1, 1, h)
+            ve_late(h)
         add_record_and_store(0, 0, LAST_CUT)
-        apply_gate(1, 0)
+        apply_gate_late(0)
         add_record_and_store(0, LAST_CUT, J)
-        apply_gate(1, 1)
+        apply_gate_late(1)
         add_record_and_store(1, 0, PART)
         add_record_and_store(1, PART, LAST_CUT)
         add_record_and_store(1, LAST_CUT, J)

@@ -52,18 +52,18 @@ def tile_list_engram_hl_tanhL_kernel(
         ps = ctx.enter_context(tc.psum_pool(name="ps", bufs=1))
 
         def tiles(name, count, shape, dtype):
-            return [sb.tile(shape, dtype, name=f"{name}{i}", align_bytes=64) for i in range(count)]
+            return [sb.tile(shape, dtype, name=f"{name}{i}", align_bytes=256) for i in range(count)]
 
         offsets = sb.tile([P, J // PER_COLUMN], U16, name="offsets")
-        tab_plane = sb.tile([P, T], U8, name="tab_plane", align_bytes=64)
-        picked_plane = sb.tile([P, J], U8, name="picked_plane", align_bytes=64)
+        tab_plane = sb.tile([P, T], U8, name="tab_plane", align_bytes=256)
+        picked_plane = sb.tile([P, J], U8, name="picked_plane", align_bytes=256)
         tab_w = tiles("tab_w", PASSES, [P, T], I32)
-        picked_first = sb.tile([P, J], U32, name="picked_first", align_bytes=64)
-        picked_last = sb.tile([P, J], U32, name="picked_last", align_bytes=64)
+        picked_first = sb.tile([P, J], U32, name="picked_first", align_bytes=256)
+        picked_last = sb.tile([P, J], U32, name="picked_last", align_bytes=256)
         picked_whole = [picked_first, picked_last]
         picked = {(a, b): picked_whole[a][:, b * PART : (b + 1) * PART] for a in range(PASSES) for b in range(PARTS)}
-        gate_whole = sb.tile([P, J], F32, name="gate_whole", align_bytes=64)
-        wk_raw = [sb.tile([P, PACK, N], F32, name=f"wk_raw{a}", tag=f"wk_raw{a}", align_bytes=64) for a in range(PASSES)]
+        gate_whole = sb.tile([P, J], F32, name="gate_whole", align_bytes=256)
+        wk_raw = [sb.tile([P, PACK, N], F32, name=f"wk_raw{a}", tag=f"wk_raw{a}", align_bytes=256) for a in range(PASSES)]
         wv_raw = tiles("wv_raw", PASSES, [P, PACK, N], F32)
         wv_hi = tiles("wv_hi", PASSES, [P, PACK, N], F32)
         wv_top = {}
@@ -75,7 +75,7 @@ def tile_list_engram_hl_tanhL_kernel(
         st_sb = tiles("st_sb", HALVES, [P, J], F32)
         r_sb = tiles("r_sb", HALVES, [P, T], F32)
         z = tiles("z", HALVES, [P, J], F32)
-        gate = [[sb.tile([P, PART], F32, name=f"gate{h}{b}", tag=f"gate{h}{b}", align_bytes=64) for b in range(PARTS)] for h in range(1)]
+        gate = [[sb.tile([P, PART], F32, name=f"gate{h}{b}", tag=f"gate{h}{b}", align_bytes=256) for b in range(PARTS)] for h in range(1)]
         prod = tiles("prod", HALVES, [P, J], F32)
         res = tiles("res", HALVES, [P, J], F32)
         ke = [[ps.tile([P, PART], F32, name=f"ke0{b}") for b in range(PARTS)]]
@@ -101,13 +101,13 @@ def tile_list_engram_hl_tanhL_kernel(
                 )
 
         def open_pair(a, first, tag):
-            pairs[(a, first)] = sb.tile([P, 2 * SLOT_VALUES], BF16, name=f"bf{a}{first}", tag=tag, align_bytes=64)
+            pairs[(a, first)] = sb.tile([P, 2 * SLOT_VALUES], BF16, name=f"bf{a}{first}", tag=tag, align_bytes=256)
 
         def open_codes(a, first, tag):
-            codes[(a, first)] = sb.tile([P, 2 * P], U32, name=f"codes{a}{first}", tag=tag, align_bytes=64)
+            codes[(a, first)] = sb.tile([P, 2 * P], U32, name=f"codes{a}{first}", tag=tag, align_bytes=256)
 
         def open_single_codes(key, tag):
-            single_codes[key] = sb.tile([P, P], U32, name=f"single_codes{key[1]}", tag=tag, align_bytes=64)
+            single_codes[key] = sb.tile([P, P], U32, name=f"single_codes{key[1]}", tag=tag, align_bytes=256)
 
         def slot_codes(a, first, count=1):
             if (a, first) in single_codes:
@@ -116,13 +116,13 @@ def tile_list_engram_hl_tanhL_kernel(
             return codes[(a, first - at)][:, at * P : (at + count) * P].bitcast(FP8X4)
 
         def open_picked(b, tag):
-            picked[(1, b)] = sb.tile([P, PART], U32, name=f"picked1{b}", tag=tag, align_bytes=64)[:]
+            picked[(1, b)] = sb.tile([P, PART], U32, name=f"picked1{b}", tag=tag, align_bytes=256)[:]
 
         def open_top(a, h, tag):
-            wv_top[HALVES * a + h] = sb.tile([P, SLOT_VALUES], BF16, name=f"top{a}{h}", tag=tag, align_bytes=64)
+            wv_top[HALVES * a + h] = sb.tile([P, SLOT_VALUES], BF16, name=f"top{a}{h}", tag=tag, align_bytes=256)
 
         def open_single(key, tag):
-            singles[key] = sb.tile([P, SLOT_VALUES], BF16, name=f"single{key[1]}", tag=tag, align_bytes=64)
+            singles[key] = sb.tile([P, SLOT_VALUES], BF16, name=f"single{key[1]}", tag=tag, align_bytes=256)
 
         def slots(a, first, count=1):
             if (a, first) in singles:

@@ -22,25 +22,22 @@ HALVES = N // P
 QUADRANTS = 4
 SCALE_ROWS = 4
 PER_COLUMN = 16
-PARTS = 2
-PART = J // PARTS
-HI_MASK = 0xFFF00000 - (1 << 32)
+PART = J // 2
+SLOT = PACK * P
 HI_PAIR_MASK = 0xFFF0FFF0 - (1 << 32)
-SLOTS = 6
-KEY = (0, 1)
-HI = (2, 4)
-LO = (3, 5)
-SLOT_VALUES = PACK * P
 LAST_CUT = 384
-RUN = 2
+VECTOR_RUN = 2
+HI_MASK = 0xFFF00000 - (1 << 32)
+SCALAR_RUN = 2
+ALIGN = 256
 
 
-def rows_walk(rows):
-    return rows.rearrange("p t (c i) -> p c t i", i=RUN)
+def rows_walk(rows, run):
+    return rows.rearrange("p t (c i) -> p c t i", i=run)
 
 
-def packed_walk(values):
-    return values.rearrange("p (c i t) -> p c t i", i=RUN, t=PACK)
+def packed_walk(values, run):
+    return values.rearrange("p (c i t) -> p c t i", i=run, t=PACK)
 
 
 def tile_list_engram_hl_tanhL_kernel(
@@ -51,47 +48,54 @@ def tile_list_engram_hl_tanhL_kernel(
         sb = ctx.enter_context(tc.tile_pool(name="sb", bufs=1))
         ps = ctx.enter_context(tc.psum_pool(name="ps", bufs=1))
 
-        def tiles(name, count, shape, dtype):
-            return [sb.tile(shape, dtype, name=f"{name}{i}", align_bytes=256) for i in range(count)]
+        def tile(name, shape, dtype, tag=None):
+            return sb.tile(shape, dtype, name=name, tag=tag or name, align_bytes=ALIGN)
 
         offsets = sb.tile([P, J // PER_COLUMN], U16, name="offsets")
-        tab_plane = sb.tile([P, T], U8, name="tab_plane", align_bytes=256)
-        picked_plane = sb.tile([P, J], U8, name="picked_plane", align_bytes=256)
-        tab_w = tiles("tab_w", PASSES, [P, T], I32)
-        picked_first = sb.tile([P, J], U32, name="picked_first", align_bytes=256)
-        picked_last = sb.tile([P, J], U32, name="picked_last", align_bytes=256)
-        picked_whole = [picked_first, picked_last]
-        picked = {(a, b): picked_whole[a][:, b * PART : (b + 1) * PART] for a in range(PASSES) for b in range(PARTS)}
-        gate_whole = sb.tile([P, J], F32, name="gate_whole", align_bytes=256)
-        wk_raw = [sb.tile([P, PACK, N], F32, name=f"wk_raw{a}", tag=f"wk_raw{a}", align_bytes=256) for a in range(PASSES)]
-        wv_raw = tiles("wv_raw", PASSES, [P, PACK, N], F32)
-        wv_hi = tiles("wv_hi", PASSES, [P, PACK, N], F32)
-        wv_top = {}
-        pairs = {}
-        singles = {}
-        single_codes = {}
-        codes = {}
-        w_plane = tiles("w_plane", PASSES, [P, SLOTS * P], U8)
-        st_sb = tiles("st_sb", HALVES, [P, J], F32)
-        r_sb = tiles("r_sb", HALVES, [P, T], F32)
-        z = tiles("z", HALVES, [P, J], F32)
-        gate = [[sb.tile([P, PART], F32, name=f"gate{h}{b}", tag=f"gate{h}{b}", align_bytes=256) for b in range(PARTS)] for h in range(1)]
-        prod = tiles("prod", HALVES, [P, J], F32)
-        res = tiles("res", HALVES, [P, J], F32)
-        ke = [[ps.tile([P, PART], F32, name=f"ke0{b}") for b in range(PARTS)]]
-        ke_whole = ps.tile([P, J], F32, name="ke1")
-        ve_whole = ps.tile([P, J], F32, name="ve0")
-        ve = [
-            [ve_whole[:, b * PART : (b + 1) * PART] for b in range(PARTS)],
-            [ps.tile([P, PART], F32, name=f"ve1{b}")[:] for b in range(PARTS)],
-        ]
+        tab_plane = tile("tab_plane", [P, T], U8)
+        picked_plane = tile("picked_plane", [P, J], U8)
+        tab_w = [tile(f"tab_w{a}", [P, T], I32) for a in range(PASSES)]
+        picked = {(a, b): tile(f"picked{a}{b}", [P, PART], U32)[:] for a in range(PASSES) for b in range(2)}
+        wk_raw = [tile(f"wk_raw{a}", [P, PACK, N], F32) for a in range(PASSES)]
+        wv_raw = [tile(f"wv_raw{a}", [P, PACK, N], F32) for a in range(PASSES)]
+        quarters = [(a, h) for a in range(PASSES) for h in range(HALVES)]
+        wk_rows = {(a, h): wk_raw[a][:, :, h * P : (h + 1) * P] for a, h in quarters}
+        wv_rows = {(a, h): wv_raw[a][:, :, h * P : (h + 1) * P] for a, h in quarters}
+        top_last = tile("top_last", [P, 2 * SLOT], BF16)
+        top = {(1, h): top_last[:, h * SLOT : (h + 1) * SLOT] for h in range(HALVES)}
+        hi_first = tile("hi_first", [P, PACK, N], F32)
+        hi_words = {(0, h): hi_first[:, :, h * P : (h + 1) * P] for h in range(HALVES)}
+        key0 = tile("key0", [P, 2 * SLOT], BF16)
+        late = tile("late", [P, SLOT], BF16)
+        key1 = [tile("key10", [P, SLOT], BF16)[:], late[:]]
+        val = {q: tile(f"val{q[0]}{q[1]}", [P, 2 * SLOT], BF16) for q in ((0, 0), (0, 1), (1, 0))}
+        hi_slots = {q: val[q][:, 0:SLOT] for q in val}
+        lo_slots = {q: val[q][:, SLOT : 2 * SLOT] for q in val}
+        hi_slots[(1, 1)] = tile("hi11", [P, SLOT], BF16)[:]
+        lo_slots[(1, 1)] = late[:]
+        key_codes = [tile(f"key_codes{a}", [P, 2 * P], U32) for a in range(PASSES)]
+        val_codes = {q: tile(f"val_codes{q[0]}{q[1]}", [P, 2 * P], U32) for q in ((0, 0), (0, 1))}
+        hi_codes_last = tile("hi_codes_last", [P, P], U32)
+        key_plane = tile("key_plane", [P, 3 * P], U8)
+        val_plane = {q: tile(f"val_plane{q[0]}{q[1]}", [P, 2 * P], U8) for q in ((0, 0), (0, 1), (1, 0), (1, 1))}
+        st_sb = [tile(f"st_sb{h}", [P, J], F32) for h in range(HALVES)]
+        r_sb = [tile(f"r_sb{h}", [P, T], F32) for h in range(HALVES)]
+        z = [tile(f"z{h}", [P, J], F32) for h in range(HALVES)]
+        gate = [[tile(f"gate{h}{b}", [P, PART], F32) for b in range(2)] for h in range(HALVES)]
+        prod = [tile(f"prod{h}", [P, J], F32) for h in range(HALVES)]
+        res = {1: tile("res1", [P, J], F32)}
+        ke = [[ps.tile([P, PART], F32, name=f"ke{h}{b}")[:] for b in range(2)] for h in range(HALVES)]
+        ve = [[ps.tile([P, PART], F32, name=f"ve{h}{b}")[:] for b in range(2)] for h in range(HALVES)]
+
+        def part(b):
+            return slice(b * PART, (b + 1) * PART)
 
         def load_words(a):
             nc.sync.dma_start(tab_w[a][:], tab_words[a].rearrange("p t i -> p (t i)").bitcast(I32))
 
-        def load_weight(dst, src, a):
-            rows = src[a * P * PACK : (a + 1) * P * PACK, :]
-            nc.sync.dma_start(dst[a][:], rows.rearrange("(p t) n -> p t n", t=PACK))
+        def load_weight(dst, src, a, n0, n1):
+            rows = src[a * P * PACK : (a + 1) * P * PACK, n0:n1]
+            nc.sync.dma_start(dst, rows.rearrange("(p t) n -> p t n", t=PACK))
 
         def load_scales():
             for quad in range(QUADRANTS):
@@ -100,112 +104,71 @@ def tile_list_engram_hl_tanhL_kernel(
                     tab_scales[:, SCALE_ROWS * quad : SCALE_ROWS * (quad + 1), :].bitcast(I32),
                 )
 
-        def open_pair(a, first, tag):
-            pairs[(a, first)] = sb.tile([P, 2 * SLOT_VALUES], BF16, name=f"bf{a}{first}", tag=tag, align_bytes=256)
-
-        def open_codes(a, first, tag):
-            codes[(a, first)] = sb.tile([P, 2 * P], U32, name=f"codes{a}{first}", tag=tag, align_bytes=256)
-
-        def open_single_codes(key, tag):
-            single_codes[key] = sb.tile([P, P], U32, name=f"single_codes{key[1]}", tag=tag, align_bytes=256)
-
-        def slot_codes(a, first, count=1):
-            if (a, first) in single_codes:
-                return single_codes[(a, first)][:].bitcast(FP8X4)
-            at = first % 2
-            return codes[(a, first - at)][:, at * P : (at + count) * P].bitcast(FP8X4)
-
-        def open_picked(b, tag):
-            picked[(1, b)] = sb.tile([P, PART], U32, name=f"picked1{b}", tag=tag, align_bytes=256)[:]
-
-        def open_top(a, h, tag):
-            wv_top[HALVES * a + h] = sb.tile([P, SLOT_VALUES], BF16, name=f"top{a}{h}", tag=tag, align_bytes=256)
-
-        def open_single(key, tag):
-            singles[key] = sb.tile([P, SLOT_VALUES], BF16, name=f"single{key[1]}", tag=tag, align_bytes=256)
-
-        def slots(a, first, count=1):
-            if (a, first) in singles:
-                return singles[(a, first)][:]
-            at = first % 2
-            return pairs[(a, first - at)][:, at * SLOT_VALUES : (at + count) * SLOT_VALUES]
-
-        def half(rows, h):
-            return rows[:, :, h * P : (h + 1) * P]
-
         def entries(j0, j1):
             return offsets[:, j0 // PER_COLUMN : j1 // PER_COLUMN]
 
-        def gather_first():
-            nc.vector.tensor_copy(picked_first[:], tab_w[0][:].bitcast(U32).indirect(offsets[:]))
-
-        def gather_words(b):
-            nc.vector.tensor_copy(picked[(1, b)], tab_w[1][:].bitcast(U32).indirect(entries(b * PART, (b + 1) * PART)))
+        def gather_words(dst, a, j0, j1):
+            nc.vector.tensor_copy(dst, tab_w[a][:].bitcast(U32).indirect(entries(j0, j1)))
 
         def gather_scales():
             nc.vector.tensor_copy(picked_plane[:], tab_plane[:].indirect(offsets[:]))
 
-        def cast_wk(a):
-            nc.scalar.copy(packed_walk(slots(a, KEY[0], HALVES)), rows_walk(wk_raw[a][:]))
+        def cast(dst, rows):
+            nc.scalar.copy(packed_walk(dst, SCALAR_RUN), rows_walk(rows, SCALAR_RUN))
 
-        def cast_wk_half(a, h, eng="s"):
-            if eng == "s":
-                nc.scalar.copy(packed_walk(slots(a, KEY[h])), rows_walk(half(wk_raw[a], h)))
-            else:
-                nc.vector.tensor_copy(packed_walk(slots(a, KEY[h])), rows_walk(half(wk_raw[a], h)))
+        def copy_top(dst, rows):
+            upper = rows.bitcast(BF16).rearrange("p t (c i e) -> p c t i e", i=SCALAR_RUN, e=2)[:, :, :, :, 1]
+            nc.scalar.copy(packed_walk(dst, SCALAR_RUN), upper)
 
-        def mask_hi(a, h):
-            nc.vector.tensor_scalar(
-                half(wv_hi[a], h).bitcast(I32), half(wv_raw[a], h).bitcast(I32), HI_MASK, None, ALU.bitwise_and
-            )
+        def mask_top(q):
+            nc.vector.tensor_scalar(hi_slots[q].bitcast(I32), top[q].bitcast(I32), HI_PAIR_MASK, None, ALU.bitwise_and)
 
-        def cast_hi(a, h):
-            nc.scalar.copy(packed_walk(slots(a, HI[h])), rows_walk(half(wv_hi[a], h)))
-
-        def make_lo(a, h):
+        def make_lo(q):
             nc.vector.tensor_tensor(
-                packed_walk(slots(a, LO[h])), rows_walk(half(wv_raw[a], h)), rows_walk(half(wv_hi[a], h)), ALU.subtract
-            )
-
-        def copy_top(a, h):
-            upper = half(wv_raw[a], h).bitcast(BF16).rearrange("p t (c i e) -> p c t i e", i=RUN, e=2)[:, :, :, :, 1]
-            nc.scalar.copy(packed_walk(wv_top[HALVES * a + h][:]), upper)
-
-        def mask_top(a, h):
-            nc.vector.tensor_scalar(
-                slots(a, HI[h]).bitcast(I32), wv_top[HALVES * a + h][:].bitcast(I32), HI_PAIR_MASK, None, ALU.bitwise_and
-            )
-
-        def make_lo_top(a, h):
-            nc.vector.tensor_tensor(
-                packed_walk(slots(a, LO[h])), rows_walk(half(wv_raw[a], h)), packed_walk(slots(a, HI[h])), ALU.subtract
-            )
-
-        def make_lo_pool(a, h):
-            nc.gpsimd.tensor_tensor(
-                slots(a, LO[h]).rearrange("p (n t) -> p n t", t=PACK),
-                half(wv_raw[a], h).rearrange("p t n -> p n t"),
-                slots(a, HI[h]).rearrange("p (n t) -> p n t", t=PACK),
+                packed_walk(lo_slots[q], VECTOR_RUN),
+                rows_walk(wv_rows[q], VECTOR_RUN),
+                packed_walk(hi_slots[q], VECTOR_RUN),
                 ALU.subtract,
             )
 
-        def plane(a, first, count=1):
-            if (a, first) == (1, KEY[1]):
-                return w_plane[a][SCALE_ROWS:P, HI[0] * P : (HI[0] + 1) * P]
-            return w_plane[a][:, first * P : (first + count) * P]
-
-        def quantise(a, first, count):
-            nc.vector.quantize_mx(
-                out=slot_codes(a, first, count),
-                scales=plane(a, first, count),
-                in_=slots(a, first, count),
+        def mask_words(t0, t1, n0, n1):
+            nc.vector.tensor_scalar(
+                hi_first[:, t0:t1, n0:n1].bitcast(I32), wv_raw[0][:, t0:t1, n0:n1].bitcast(I32), HI_MASK, None, ALU.bitwise_and
             )
 
-        def mx_pass(acc, a, slot, words, j0, j1, start, stop):
+        def make_lo_from_words(q):
+            nc.vector.tensor_tensor(
+                packed_walk(lo_slots[q], VECTOR_RUN),
+                rows_walk(wv_rows[q], VECTOR_RUN),
+                rows_walk(hi_words[q], VECTOR_RUN),
+                ALU.subtract,
+            )
+
+        def make_lo_on_pool(q):
+            nc.gpsimd.tensor_tensor(
+                lo_slots[q].rearrange("p (n t) -> p n t", t=PACK),
+                wv_rows[q].rearrange("p t n -> p n t"),
+                hi_slots[q].rearrange("p (n t) -> p n t", t=PACK),
+                ALU.subtract,
+            )
+
+        def key_scales(a, h, count=1):
+            if (a, h) == (1, 1):
+                return val_plane[(1, 0)][SCALE_ROWS:P, 0:P]
+            at = (HALVES * a + h) * P
+            return key_plane[:, at : at + count * P]
+
+        def quantise(codes, scales, values):
+            nc.vector.quantize_mx(out=codes.bitcast(FP8X4), scales=scales, in_=values)
+
+        def quantise_val(q):
+            quantise(val_codes[q][:], val_plane[q][:], val[q][:])
+
+        def mx_pass(acc, a, codes, scales, words, j0, j1, start, stop):
             nc.tensor.matmul_mx(
                 out=acc,
-                lhsT=slot_codes(a, slot),
-                lhsT_scale=plane(a, slot),
+                lhsT=codes.bitcast(FP8X4),
+                lhsT_scale=scales,
                 rhs=words.bitcast(FP8X4),
                 rhs_scale=picked_plane[SCALE_ROWS * a : P, j0:j1],
                 start=start,
@@ -213,45 +176,24 @@ def tile_list_engram_hl_tanhL_kernel(
             )
 
         def ke_pass(a, h, b):
-            mx_pass(ke[h][b][:], a, KEY[h], picked[(a, b)], b * PART, (b + 1) * PART, a == 0, a == PASSES - 1)
+            codes = key_codes[a][:, h * P : (h + 1) * P]
+            mx_pass(ke[h][b], a, codes, key_scales(a, h), picked[(a, b)], b * PART, (b + 1) * PART, a == 0, a == PASSES - 1)
 
-        def ve_whole_first():
-            mx_pass(ve_whole[:], 0, HI[0], picked_first[:], 0, J, True, False)
-            mx_pass(ve_whole[:], 0, LO[0], picked_first[:], 0, J, False, False)
+        def ve_pass(q, s, b, start, stop):
+            cols = slice(s * P, (s + 1) * P)
+            codes = val_codes[q][:, cols]
+            mx_pass(ve[q[1]][b], q[0], codes, val_plane[q][:, cols], picked[(q[0], b)], b * PART, (b + 1) * PART, start, stop)
 
-        def ve_late(b):
-            j0, j1 = b * PART, (b + 1) * PART
-            mx_pass(ve[1][b], 1, LO[1], picked[(1, b)], j0, j1, False, False)
-            mx_pass(ve[1][b], 1, HI[1], picked[(1, b)], j0, j1, False, True)
-
-        def ke_whole_pass(a):
-            mx_pass(ke_whole[:], a, KEY[1], picked_whole[a][:], 0, J, a == 0, a == PASSES - 1)
-
-        def ve_whole_last():
-            mx_pass(ve_whole[:], 1, HI[0], picked_last[:], 0, J, False, False)
-            mx_pass(ve_whole[:], 1, LO[0], picked_last[:], 0, J, False, True)
-
-        def make_gate_whole():
-            nc.vector.tensor_tensor(z[1][:], st_sb[1][:], ke_whole[:], ALU.mult)
-            nc.scalar.activation(gate_whole[:], z[1][:], ACT.Tanh)
-
-        def apply_gate_late(b):
-            cols = slice(b * PART, (b + 1) * PART)
-            nc.vector.tensor_tensor(prod[1][:, cols], gate_whole[:, cols], ve[1][b], ALU.mult)
-
-        def ve_part(a, h, b):
-            j0, j1 = b * PART, (b + 1) * PART
-            mx_pass(ve[h][b], a, HI[h], picked[(a, b)], j0, j1, a == 0, False)
-            mx_pass(ve[h][b], a, LO[h], picked[(a, b)], j0, j1, False, a == PASSES - 1 and (h == 1 or b == PARTS - 1))
+        def ve_last(codes, s, b, stop):
+            scales = val_plane[(1, 1)][:, s * P : (s + 1) * P]
+            mx_pass(ve[1][b], 1, codes, scales, picked[(1, b)], b * PART, (b + 1) * PART, False, stop)
 
         def make_gate(h, b):
-            cols = slice(b * PART, (b + 1) * PART)
-            nc.vector.tensor_tensor(z[h][:, cols], st_sb[h][:, cols], ke[h][b][:], ALU.mult)
-            nc.scalar.activation(gate[h][b][:], z[h][:, cols], ACT.Tanh)
+            nc.vector.tensor_tensor(z[h][:, part(b)], st_sb[h][:, part(b)], ke[h][b], ALU.mult)
+            nc.scalar.activation(gate[h][b][:], z[h][:, part(b)], ACT.Tanh)
 
         def apply_gate(h, b):
-            cols = slice(b * PART, (b + 1) * PART)
-            nc.vector.tensor_tensor(prod[h][:, cols], gate[h][b][:], ve[h][b], ALU.mult)
+            nc.vector.tensor_tensor(prod[h][:, part(b)], gate[h][b][:], ve[h][b], ALU.mult)
 
         def add_record_and_store(h, j0, j1):
             nc.vector.tensor_tensor(res[h][:, j0:j1], r_sb[h][:].indirect(entries(j0, j1)), prod[h][:, j0:j1], ALU.add)
@@ -259,86 +201,76 @@ def tile_list_engram_hl_tanhL_kernel(
 
         nc.vector.memset(tab_plane[:].bitcast(I32), 0)
 
-        load_words(0)
+        first_rows = wv[0 : P * PACK, :].rearrange("(p t) n -> p t n", t=PACK)
+        for t0 in range(0, PACK, 2):
+            nc.sync.dma_start(wv_raw[0][:, t0 : t0 + 2, :], first_rows[:, t0 : t0 + 2, :])
         nc.sync.dma_start(offsets[:], offs)
         load_scales()
-        load_weight(wv_raw, wv, 0)
-        load_weight(wv_raw, wv, 1)
-        load_weight(wk_raw, wk, 0)
-        load_weight(wk_raw, wk, 1)
+        load_words(0)
+        load_weight(wv_raw[1][:], wv, 1, 0, N)
+        for a in range(PASSES):
+            load_weight(wk_raw[a][:], wk, a, 0, N)
         load_words(1)
-        nc.sync.dma_start(st_sb[0][:], st[0:P, :])
-        nc.sync.dma_start(st_sb[1][:], st[P : 2 * P, :])
-        nc.sync.dma_start(r_sb[0][:], rT[0:P, :])
-        nc.sync.dma_start(r_sb[1][:], rT[P : 2 * P, :])
+        for h in range(HALVES):
+            nc.sync.dma_start(st_sb[h][:], st[h * P : (h + 1) * P, :])
+        for h in range(HALVES):
+            nc.sync.dma_start(r_sb[h][:], rT[h * P : (h + 1) * P, :])
 
-        open_codes(0, 0, "c00")
-        open_codes(0, 2, "c02")
-        open_codes(0, 4, "c04")
-        open_codes(1, 0, "c10")
-        open_codes(1, 2, "c12")
-        open_single_codes((1, 4), "c14")
-        open_pair(0, 0, "k0")
-        open_single((1, 0), "k10")
-        open_single((1, 1), "k11")
-        open_pair(0, 2, "v00")
-        open_pair(0, 4, "v01")
-        open_pair(1, 2, "v10")
-        open_single((1, 4), "hi11")
-        open_top(0, 0, "t00")
-        open_top(0, 1, "t01")
-        open_top(1, 0, "t10")
-        open_top(1, 1, "t11")
-        gather_first()
+        mask_words(0, 2, 0, N)
+        for h in range(HALVES):
+            mask_words(2, PACK, h * P, (h + 1) * P)
+            cast(hi_slots[(0, h)], hi_words[(0, h)])
+        copy_top(top_last[:], wv_raw[1][:])
+        cast(key0[:], wk_raw[0][:])
+        for h in range(HALVES):
+            cast(key1[h], wk_rows[(1, h)])
+        for h in range(HALVES):
+            make_lo_from_words((0, h))
         gather_scales()
         for h in range(HALVES):
-            copy_top(0, h)
+            quantise_val((0, h))
+        for b in range(2):
+            gather_words(picked[(0, b)], 0, b * PART, (b + 1) * PART)
+            for h in range(HALVES):
+                for s in range(2):
+                    ve_pass((0, h), s, b, s == 0, False)
         for h in range(HALVES):
-            copy_top(1, h)
-        cast_wk(0)
+            mask_top((1, h))
+        make_lo((1, 0))
+        quantise(hi_codes_last[:], val_plane[(1, 1)][:, 0:P], hi_slots[(1, 1)])
+        quantise(key_codes[0][:], key_scales(0, 0, HALVES), key0[:])
         for h in range(HALVES):
-            cast_wk_half(1, h)
-        mask_top(0, 0)
-        make_lo_top(0, 0)
-        mask_top(0, 1)
-        quantise(0, HI[0], 2)
-        make_lo_top(0, 1)
-        mask_top(1, 0)
-        quantise(0, HI[1], 2)
-        ve_whole_first()
+            for b in range(2):
+                ke_pass(0, h, b)
+        val_codes[(1, 0)] = tile("val_codes10", [P, 2 * P], U32, tag="wk_raw0")
+        quantise_val((1, 0))
+        gather_words(picked[(1, 0)], 1, 0, PART)
+        quantise(key_codes[1][:, 0:P], key_scales(1, 0), key1[0])
+        gather_words(picked[(1, 1)], 1, PART, J)
+        quantise(key_codes[1][:, P : 2 * P], key_scales(1, 1), key1[1])
+        make_lo_on_pool((1, 1))
         for h in range(HALVES):
-            ve_part(0, 1, h)
-        make_lo_top(1, 0)
-        mask_top(1, 1)
-        quantise(1, HI[0], 2)
-        quantise(1, HI[1], 1)
-        quantise(0, KEY[0], 2)
+            for b in range(2):
+                ke_pass(1, h, b)
+        for b in range(2):
+            for s in range(2):
+                ve_pass((1, 0), s, b, False, s == 1)
+        for b in range(2):
+            ve_last(hi_codes_last[:], 0, b, False)
         for h in range(HALVES):
-            ke_pass(0, 0, h)
-        ke_whole_pass(0)
-        gather_words(0)
-        quantise(1, KEY[0], 1)
-        gather_words(1)
-        quantise(1, KEY[1], 1)
-        open_single((1, 5), "k11")
-        make_lo_pool(1, 1)
-        for h in range(HALVES):
-            ke_pass(1, 0, h)
-        ke_whole_pass(1)
-        ve_whole_last()
-        for h in range(HALVES):
-            make_gate(0, h)
-        make_gate_whole()
-        apply_gate(0, 0)
-        apply_gate(0, 1)
-        open_single_codes((1, 5), "gate00")
-        quantise(1, LO[1], 1)
-        for h in range(HALVES):
-            ve_late(h)
-        add_record_and_store(0, 0, LAST_CUT)
-        apply_gate_late(0)
-        add_record_and_store(0, LAST_CUT, J)
-        apply_gate_late(1)
+            for b in range(2):
+                make_gate(h, b)
+        for b in range(2):
+            apply_gate(0, b)
+        lo_codes_last = tile("lo_codes_last", [P, P], U32, tag="gate00")
+        quantise(lo_codes_last[:], val_plane[(1, 1)][:, P : 2 * P], lo_slots[(1, 1)])
+        for b in range(2):
+            ve_last(lo_codes_last[:], 1, b, True)
+        res[0] = tile("res0", [P, J], F32, tag="wv_raw1")
+        for b in range(2):
+            add_record_and_store(0, b * PART, (b + 1) * PART)
+        for b in range(2):
+            apply_gate(1, b)
         add_record_and_store(1, 0, PART)
         add_record_and_store(1, PART, LAST_CUT)
         add_record_and_store(1, LAST_CUT, J)

@@ -75,7 +75,6 @@ def tile_list_engram_hl_tanhL_kernel(
         lo_slots[(1, 1)] = late[:]
         key_codes = [tile(f"key_codes{a}", [P, 2 * P], U32) for a in range(PASSES)]
         val_codes = {q: tile(f"val_codes{q[0]}{q[1]}", [P, 2 * P], U32) for q in ((0, 0), (0, 1))}
-        hi_codes_last = tile("hi_codes_last", [P, P], U32)
         key_plane = tile("key_plane", [P, 3 * P], U8)
         val_plane = {q: tile(f"val_plane{q[0]}{q[1]}", [P, 2 * P], U8) for q in ((0, 0), (0, 1), (1, 0), (1, 1))}
         st_sb = [tile(f"st_sb{h}", [P, J], F32) for h in range(HALVES)]
@@ -206,8 +205,8 @@ def tile_list_engram_hl_tanhL_kernel(
             nc.sync.dma_start(wv_raw[0][:, t0 : t0 + 2, :], first_rows[:, t0 : t0 + 2, :])
         nc.sync.dma_start(offsets[:], offs)
         load_scales()
-        load_words(0)
         load_weight(wv_raw[1][:], wv, 1, 0, N)
+        load_words(0)
         for a in range(PASSES):
             load_weight(wk_raw[a][:], wk, a, 0, N)
         load_words(1)
@@ -229,15 +228,15 @@ def tile_list_engram_hl_tanhL_kernel(
         gather_scales()
         for h in range(HALVES):
             quantise_val((0, h))
+        gather_words(picked[(0, 0)], 0, 0, PART)
+        for h in range(HALVES):
+            mask_top((1, h))
+        gather_words(picked[(0, 1)], 0, PART, J)
         for b in range(2):
-            gather_words(picked[(0, b)], 0, b * PART, (b + 1) * PART)
             for h in range(HALVES):
                 for s in range(2):
                     ve_pass((0, h), s, b, s == 0, False)
-        for h in range(HALVES):
-            mask_top((1, h))
         make_lo((1, 0))
-        quantise(hi_codes_last[:], val_plane[(1, 1)][:, 0:P], hi_slots[(1, 1)])
         quantise(key_codes[0][:], key_scales(0, 0, HALVES), key0[:])
         for h in range(HALVES):
             for b in range(2):
@@ -248,6 +247,8 @@ def tile_list_engram_hl_tanhL_kernel(
         quantise(key_codes[1][:, 0:P], key_scales(1, 0), key1[0])
         gather_words(picked[(1, 1)], 1, PART, J)
         quantise(key_codes[1][:, P : 2 * P], key_scales(1, 1), key1[1])
+        hi_codes_last = tile("hi_codes_last", [P, P], U32, tag="wk_raw1")
+        quantise(hi_codes_last[:], val_plane[(1, 1)][:, 0:P], hi_slots[(1, 1)])
         make_lo_on_pool((1, 1))
         for h in range(HALVES):
             for b in range(2):

@@ -28,6 +28,8 @@ HI_PAIR_MASK = 0xFFF0FFF0 - (1 << 32)
 LAST_CUT = 384
 VECTOR_RUN = 2
 HI_MASK = 0xFFF00000 - (1 << 32)
+SIGN_BIT = -(1 << 31)
+BLOCK = 32
 SCALAR_RUN = 2
 ALIGN = 256
 
@@ -83,7 +85,14 @@ def tile_list_engram_hl_tanhL_kernel(
         gate = [[tile(f"gate{h}{b}", [P, PART], F32) for b in range(2)] for h in range(HALVES)]
         prod = [tile(f"prod{h}", [P, J], F32) for h in range(HALVES)]
         res = {1: tile("res1", [P, J], F32)}
-        ke = [[ps.tile([P, PART], F32, name=f"ke{h}{b}")[:] for b in range(2)] for h in range(HALVES)]
+        ones = tile("ones", [P, P], F32)
+        column = tile("column", [P, P], F32)
+        row = tile("row", [P, BLOCK], F32)
+        identity = tile("identity", [P, P], F32)
+        turned = tile("turned", [P, SLOT], BF16)
+        turned_sum = ps.tile([P, PACK, P], F32, name="turned_sum", tag="bank_a")
+        turned_back = ps.tile([P, 2, P], F32, name="turned_back", tag="bank_b")
+        ke = [[ps.tile([P, PART], F32, name=f"ke0{b}")[:] for b in range(2)]]
         ve = [[ps.tile([P, PART], F32, name=f"ve{h}{b}")[:] for b in range(2)] for h in range(HALVES)]
 
         def part(b):
@@ -130,9 +139,43 @@ def tile_list_engram_hl_tanhL_kernel(
                 ALU.subtract,
             )
 
-        def mask_words(t0, t1, n0, n1):
+        def mask_words(q):
             nc.vector.tensor_scalar(
-                hi_first[:, t0:t1, n0:n1].bitcast(I32), wv_raw[0][:, t0:t1, n0:n1].bitcast(I32), HI_MASK, None, ALU.bitwise_and
+                hi_words[q].bitcast(I32), wv_rows[q].bitcast(I32), HI_MASK, SIGN_BIT, ALU.bitwise_and, ALU.bitwise_xor
+            )
+
+        def cast_negated(dst, rows):
+            nc.scalar.activation(packed_walk(dst, SCALAR_RUN), rows_walk(rows, SCALAR_RUN), ACT.Copy, scale=-1.0)
+
+        def make_identity_on_vector():
+            nc.vector.memset(ones[:], 1.0)
+            nc.vector.tensor_tensor_scan(column[:], ones[:], ones[:], 0.0, ALU.mult, ALU.add)
+            nc.vector.transpose(row[:], column[:, 0:BLOCK])
+            for quad in range(QUADRANTS):
+                rows = slice(BLOCK * quad, BLOCK * (quad + 1))
+                nc.vector.tensor_scalar(
+                    identity[rows, :], column[rows, :], row[rows, 0:1], float(BLOCK * quad), ALU.subtract, ALU.is_equal
+                )
+
+        def turn(acc, source, start, stop):
+            nc.tensor.matmul(acc, source, identity[:], start=start, stop=stop, is_transpose=True)
+
+        def make_lo_by_transposes(q):
+            for t in range(PACK):
+                turn(turned_sum[:, t, :], wv_rows[q][:, t, :], t == 0, False)
+            for t in range(PACK):
+                turn(turned_sum[:, t, :], hi_words[q][:, t, :], False, t == PACK - 1)
+            nc.scalar.copy(
+                turned[:].rearrange("n (u p e) -> n u p e", u=2, e=2),
+                turned_sum[:].rearrange("n (u e) p -> n u p e", e=2),
+            )
+            words = turned[:].bitcast(F32)
+            for u in range(2):
+                turn(turned_back[:, u, :], words[:, u * P : (u + 1) * P], True, True)
+
+        def fetch_lo(q):
+            nc.scalar.copy(
+                lo_slots[q].bitcast(F32).rearrange("p (n u) -> p n u", u=2), turned_back[:].rearrange("p u n -> p n u")
             )
 
         def make_lo_from_words(q):
@@ -140,7 +183,7 @@ def tile_list_engram_hl_tanhL_kernel(
                 packed_walk(lo_slots[q], VECTOR_RUN),
                 rows_walk(wv_rows[q], VECTOR_RUN),
                 rows_walk(hi_words[q], VECTOR_RUN),
-                ALU.subtract,
+                ALU.add,
             )
 
         def make_lo_on_pool(q):
@@ -200,9 +243,8 @@ def tile_list_engram_hl_tanhL_kernel(
 
         nc.vector.memset(tab_plane[:].bitcast(I32), 0)
 
-        first_rows = wv[0 : P * PACK, :].rearrange("(p t) n -> p t n", t=PACK)
-        for t0 in range(0, PACK, 2):
-            nc.sync.dma_start(wv_raw[0][:, t0 : t0 + 2, :], first_rows[:, t0 : t0 + 2, :])
+        make_identity_on_vector()
+        load_weight(wv_raw[0][:], wv, 0, 0, N)
         nc.sync.dma_start(offsets[:], offs)
         load_scales()
         load_weight(wv_raw[1][:], wv, 1, 0, N)
@@ -215,29 +257,31 @@ def tile_list_engram_hl_tanhL_kernel(
         for h in range(HALVES):
             nc.sync.dma_start(r_sb[h][:], rT[h * P : (h + 1) * P, :])
 
-        mask_words(0, 2, 0, N)
-        for h in range(HALVES):
-            mask_words(2, PACK, h * P, (h + 1) * P)
-            cast(hi_slots[(0, h)], hi_words[(0, h)])
+        for h in reversed(range(HALVES)):
+            mask_words((0, h))
+            cast_negated(hi_slots[(0, h)], hi_words[(0, h)])
+        make_lo_by_transposes((0, 1))
         copy_top(top_last[:], wv_raw[1][:])
+        fetch_lo((0, 1))
         cast(key0[:], wk_raw[0][:])
         for h in range(HALVES):
             cast(key1[h], wk_rows[(1, h)])
-        for h in range(HALVES):
-            make_lo_from_words((0, h))
+        make_lo_from_words((0, 0))
         gather_scales()
-        for h in range(HALVES):
-            quantise_val((0, h))
-        gather_words(picked[(0, 0)], 0, 0, PART)
+        quantise_val((0, 0))
+        for b in range(2):
+            gather_words(picked[(0, b)], 0, b * PART, (b + 1) * PART)
+            for s in range(2):
+                ve_pass((0, 0), s, b, s == 0, False)
         for h in range(HALVES):
             mask_top((1, h))
-        gather_words(picked[(0, 1)], 0, PART, J)
+        quantise_val((0, 1))
         for b in range(2):
-            for h in range(HALVES):
-                for s in range(2):
-                    ve_pass((0, h), s, b, s == 0, False)
+            for s in range(2):
+                ve_pass((0, 1), s, b, s == 0, False)
         make_lo((1, 0))
         quantise(key_codes[0][:], key_scales(0, 0, HALVES), key0[:])
+        ke.append([ps.tile([P, PART], F32, name=f"ke1{b}", tag=tag)[:] for b, tag in enumerate(("bank_a", "bank_b"))])
         for h in range(HALVES):
             for b in range(2):
                 ke_pass(0, h, b)

@@ -27,10 +27,11 @@ SLOT = PACK * P
 HI_PAIR_MASK = 0xFFF0FFF0 - (1 << 32)
 LAST_CUT = 384
 VECTOR_RUN = 2
+KEPT = 16
 HI_MASK = 0xFFF00000 - (1 << 32)
 SIGN_BIT = -(1 << 31)
 BLOCK = 32
-SCALAR_RUN = 2
+SCALAR_RUN = 4
 ALIGN = 256
 
 
@@ -68,13 +69,13 @@ def tile_list_engram_hl_tanhL_kernel(
         hi_first = tile("hi_first", [P, PACK, N], F32)
         hi_words = {(0, h): hi_first[:, :, h * P : (h + 1) * P] for h in range(HALVES)}
         key0 = tile("key0", [P, 2 * SLOT], BF16)
-        late = tile("late", [P, SLOT], BF16)
-        key1 = [tile("key10", [P, SLOT], BF16)[:], late[:]]
+        late = tile("late", [P, SLOT + KEPT * PACK], BF16)
+        key1 = [tile("key10", [P, SLOT], BF16)[:], late[:, KEPT * PACK :]]
         val = {q: tile(f"val{q[0]}{q[1]}", [P, 2 * SLOT], BF16) for q in ((0, 0), (0, 1), (1, 0))}
         hi_slots = {q: val[q][:, 0:SLOT] for q in val}
         lo_slots = {q: val[q][:, SLOT : 2 * SLOT] for q in val}
         hi_slots[(1, 1)] = tile("hi11", [P, SLOT], BF16)[:]
-        lo_slots[(1, 1)] = late[:]
+        lo_slots[(1, 1)] = late[:, 0:SLOT]
         key_codes = [tile(f"key_codes{a}", [P, 2 * P], U32) for a in range(PASSES)]
         val_codes = {q: tile(f"val_codes{q[0]}{q[1]}", [P, 2 * P], U32) for q in ((0, 0), (0, 1))}
         key_plane = tile("key_plane", [P, 3 * P], U8)
@@ -186,11 +187,19 @@ def tile_list_engram_hl_tanhL_kernel(
                 ALU.add,
             )
 
+        def make_lo_kept(q):
+            nc.vector.tensor_tensor(
+                packed_walk(lo_slots[q][:, 0 : KEPT * PACK], VECTOR_RUN),
+                rows_walk(wv_rows[q][:, :, 0:KEPT], VECTOR_RUN),
+                packed_walk(hi_slots[q][:, 0 : KEPT * PACK], VECTOR_RUN),
+                ALU.subtract,
+            )
+
         def make_lo_on_pool(q):
             nc.gpsimd.tensor_tensor(
-                lo_slots[q].rearrange("p (n t) -> p n t", t=PACK),
-                wv_rows[q].rearrange("p t n -> p n t"),
-                hi_slots[q].rearrange("p (n t) -> p n t", t=PACK),
+                lo_slots[q][:, KEPT * PACK :].rearrange("p (n t) -> p n t", t=PACK),
+                wv_rows[q][:, :, KEPT:].rearrange("p t n -> p n t"),
+                hi_slots[q][:, KEPT * PACK :].rearrange("p (n t) -> p n t", t=PACK),
                 ALU.subtract,
             )
 
@@ -280,6 +289,7 @@ def tile_list_engram_hl_tanhL_kernel(
             for s in range(2):
                 ve_pass((0, 1), s, b, s == 0, False)
         make_lo((1, 0))
+        make_lo_kept((1, 1))
         quantise(key_codes[0][:], key_scales(0, 0, HALVES), key0[:])
         ke.append([ps.tile([P, PART], F32, name=f"ke1{b}", tag=tag)[:] for b, tag in enumerate(("bank_a", "bank_b"))])
         for h in range(HALVES):

@@ -140,9 +140,14 @@ def tile_list_engram_hl_tanhL_kernel(
                 ALU.subtract,
             )
 
-        def mask_words(q):
+        def mask_words(q, t0, t1):
             nc.vector.tensor_scalar(
-                hi_words[q].bitcast(I32), wv_rows[q].bitcast(I32), HI_MASK, SIGN_BIT, ALU.bitwise_and, ALU.bitwise_xor
+                hi_words[q][:, t0:t1, :].bitcast(I32),
+                wv_rows[q][:, t0:t1, :].bitcast(I32),
+                HI_MASK,
+                SIGN_BIT,
+                ALU.bitwise_and,
+                ALU.bitwise_xor,
             )
 
         def cast_negated(dst, rows):
@@ -266,8 +271,10 @@ def tile_list_engram_hl_tanhL_kernel(
         for h in range(HALVES):
             nc.sync.dma_start(r_sb[h][:], rT[h * P : (h + 1) * P, :])
 
-        for h in reversed(range(HALVES)):
-            mask_words((0, h))
+        mask_words((0, 1), 0, 2)
+        mask_words((0, 0), 0, PACK)
+        mask_words((0, 1), 2, PACK)
+        for h in range(HALVES):
             cast_negated(hi_slots[(0, h)], hi_words[(0, h)])
         make_lo_by_transposes((0, 1))
         copy_top(top_last[:], wv_raw[1][:])

from contextlib import ExitStack

import concourse.mybir as mybir

K, N, T, J = 1024, 256, 1024, 512
FLOPS = 2 * 3 * K * N * J

F32 = mybir.dt.float32
BF16 = mybir.dt.bfloat16
I32 = mybir.dt.int32
U32 = mybir.dt.uint32
U16 = mybir.dt.uint16
U8 = mybir.dt.uint8
FP8X4 = mybir.dt.float8_e4m3fn_x4
ALU = mybir.AluOpType
ACT = mybir.ActivationFunctionType

P = 128
PACK = 4
PASSES = K // (P * PACK)
HALVES = N // P
QUADRANTS = 4
SCALE_ROWS = 4
PER_COLUMN = 16
PART = J // 2
SLOT = PACK * P
HI_PAIR_MASK = 0xFFF0FFF0 - (1 << 32)
LAST_CUT = 384
VECTOR_RUN = 2
KEPT = 16
HI_MASK = 0xFFF00000 - (1 << 32)
SIGN_BIT = -(1 << 31)
BLOCK = 32
SCALAR_RUN = 4
ALIGN = 256


def rows_walk(rows, run):
    return rows.rearrange("p t (c i) -> p c t i", i=run)


def packed_walk(values, run):
    return values.rearrange("p (c i t) -> p c t i", i=run, t=PACK)


def tile_list_engram_hl_tanhL_kernel(
    tc, tab_words, tab_scales, wk, wv, st, rT, offs, out
):
    nc = tc.nc
    with ExitStack() as ctx:
        sb = ctx.enter_context(tc.tile_pool(name="sb", bufs=1))
        ps = ctx.enter_context(tc.psum_pool(name="ps", bufs=1))

        def tile(name, shape, dtype, tag=None):
            return sb.tile(shape, dtype, name=name, tag=tag or name, align_bytes=ALIGN)

        offsets = sb.tile([P, J // PER_COLUMN], U16, name="offsets")
        tab_plane = tile("tab_plane", [P, T], U8)
        picked_plane = tile("picked_plane", [P, J], U8)
        tab_w = [tile(f"tab_w{a}", [P, T], I32) for a in range(PASSES)]
        picked = {(a, b): tile(f"picked{a}{b}", [P, PART], U32)[:] for a in range(PASSES) for b in range(2)}
        wk_raw = [tile(f"wk_raw{a}", [P, PACK, N], F32) for a in range(PASSES)]
        wv_raw = [tile(f"wv_raw{a}", [P, PACK, N], F32) for a in range(PASSES)]
        quarters = [(a, h) for a in range(PASSES) for h in range(HALVES)]
        wk_rows = {(a, h): wk_raw[a][:, :, h * P : (h + 1) * P] for a, h in quarters}
        wv_rows = {(a, h): wv_raw[a][:, :, h * P : (h + 1) * P] for a, h in quarters}
        top_last = tile("top_last", [P, 2 * SLOT], BF16)
        top = {(1, h): top_last[:, h * SLOT : (h + 1) * SLOT] for h in range(HALVES)}
        hi_first = tile("hi_first", [P, PACK, N], F32)
        hi_words = {(0, h): hi_first[:, :, h * P : (h + 1) * P] for h in range(HALVES)}
        key0 = tile("key0", [P, 2 * SLOT], BF16)
        late = tile("late", [P, SLOT + KEPT * PACK], BF16)
        key1 = [tile("key10", [P, SLOT], BF16)[:], late[:, KEPT * PACK :]]
        val = {q: tile(f"val{q[0]}{q[1]}", [P, 2 * SLOT], BF16) for q in ((0, 0), (0, 1), (1, 0))}
        hi_slots = {q: val[q][:, 0:SLOT] for q in val}
        lo_slots = {q: val[q][:, SLOT : 2 * SLOT] for q in val}
        hi_slots[(1, 1)] = tile("hi11", [P, SLOT], BF16)[:]
        lo_slots[(1, 1)] = late[:, 0:SLOT]
        key_codes = [tile(f"key_codes{a}", [P, 2 * P], U32) for a in range(PASSES)]
        val_codes = {q: tile(f"val_codes{q[0]}{q[1]}", [P, 2 * P], U32) for q in ((0, 0), (0, 1))}
        key_plane = tile("key_plane", [P, 3 * P], U8)
        val_plane = {q: tile(f"val_plane{q[0]}{q[1]}", [P, 2 * P], U8) for q in ((0, 0), (0, 1), (1, 0), (1, 1))}
        st_sb = [tile(f"st_sb{h}", [P, J], F32) for h in range(HALVES)]
        r_sb = [tile(f"r_sb{h}", [P, T], F32) for h in range(HALVES)]
        z = [tile(f"z{h}", [P, J], F32) for h in range(HALVES)]
        gate = [[tile(f"gate{h}{b}", [P, PART], F32) for b in range(2)] for h in range(HALVES)]
        prod = [tile(f"prod{h}", [P, J], F32) for h in range(HALVES)]
        res = {1: tile("res1", [P, J], F32)}
        ones = tile("ones", [P, P], F32)
        column = tile("column", [P, P], F32)
        row = tile("row", [P, BLOCK], F32)
        identity = tile("identity", [P, P], F32)
        turned = tile("turned", [P, SLOT], BF16)
        turned_sum = ps.tile([P, PACK, P], F32, name="turned_sum", tag="bank_a")
        turned_back = ps.tile([P, 2, P], F32, name="turned_back", tag="bank_b")
        ke = [[ps.tile([P, PART], F32, name=f"ke0{b}")[:] for b in range(2)]]
        ve = [[ps.tile([P, PART], F32, name=f"ve{h}{b}")[:] for b in range(2)] for h in range(HALVES)]

        def part(b):
            return slice(b * PART, (b + 1) * PART)

        def load_words(a):
            nc.sync.dma_start(tab_w[a][:], tab_words[a].rearrange("p t i -> p (t i)").bitcast(I32))

        def load_weight(dst, src, a, n0, n1):
            rows = src[a * P * PACK : (a + 1) * P * PACK, n0:n1]
            nc.sync.dma_start(dst, rows.rearrange("(p t) n -> p t n", t=PACK))

        def load_scales():
            for quad in range(QUADRANTS):
                nc.sync.dma_start(
                    tab_plane[32 * quad : 32 * quad + SCALE_ROWS * PASSES, :].bitcast(I32),
                    tab_scales[:, SCALE_ROWS * quad : SCALE_ROWS * (quad + 1), :].bitcast(I32),
                )

        def entries(j0, j1):
            return offsets[:, j0 // PER_COLUMN : j1 // PER_COLUMN]

        def gather_words(dst, a, j0, j1):
            nc.vector.tensor_copy(dst, tab_w[a][:].bitcast(U32).indirect(entries(j0, j1)))

        def gather_scales():
            nc.vector.tensor_copy(picked_plane[:], tab_plane[:].indirect(offsets[:]))

        def cast(dst, rows):
            nc.scalar.copy(packed_walk(dst, SCALAR_RUN), rows_walk(rows, SCALAR_RUN))

        def copy_top(dst, rows):
            upper = rows.bitcast(BF16).rearrange("p t (c i e) -> p c t i e", i=SCALAR_RUN, e=2)[:, :, :, :, 1]
            nc.scalar.copy(packed_walk(dst, SCALAR_RUN), upper)

        def mask_top(q):
            nc.vector.tensor_scalar(hi_slots[q].bitcast(I32), top[q].bitcast(I32), HI_PAIR_MASK, None, ALU.bitwise_and)

        def make_lo(q):
            nc.vector.tensor_tensor(
                packed_walk(lo_slots[q], VECTOR_RUN),
                rows_walk(wv_rows[q], VECTOR_RUN),
                packed_walk(hi_slots[q], VECTOR_RUN),
                ALU.subtract,
            )

        def mask_words(q, t0, t1):
            nc.vector.tensor_scalar(
                hi_words[q][:, t0:t1, :].bitcast(I32),
                wv_rows[q][:, t0:t1, :].bitcast(I32),
                HI_MASK,
                SIGN_BIT,
                ALU.bitwise_and,
                ALU.bitwise_xor,
            )

        def cast_negated(dst, rows):
            nc.scalar.activation(packed_walk(dst, SCALAR_RUN), rows_walk(rows, SCALAR_RUN), ACT.Copy, scale=-1.0)

        def make_identity_on_vector():
            nc.vector.memset(ones[:], 1.0)
            nc.vector.tensor_tensor_scan(column[:], ones[:], ones[:], 0.0, ALU.mult, ALU.add)
            nc.vector.transpose(row[:], column[:, 0:BLOCK])
            for quad in range(QUADRANTS):
                rows = slice(BLOCK * quad, BLOCK * (quad + 1))
                nc.vector.tensor_scalar(
                    identity[rows, :], column[rows, :], row[rows, 0:1], float(BLOCK * quad), ALU.subtract, ALU.is_equal
                )

        def turn(acc, source, start, stop):
            nc.tensor.matmul(acc, source, identity[:], start=start, stop=stop, is_transpose=True)

        def make_lo_by_transposes(q):
            for t in range(PACK):
                turn(turned_sum[:, t, :], wv_rows[q][:, t, :], t == 0, False)
            for t in range(PACK):
                turn(turned_sum[:, t, :], hi_words[q][:, t, :], False, t == PACK - 1)
            nc.scalar.copy(
                turned[:].rearrange("n (u p e) -> n u p e", u=2, e=2),
                turned_sum[:].rearrange("n (u e) p -> n u p e", e=2),
            )
            words = turned[:].bitcast(F32)
            for u in range(2):
                turn(turned_back[:, u, :], words[:, u * P : (u + 1) * P], True, True)

        def fetch_lo(q):
            nc.scalar.copy(
                lo_slots[q].bitcast(F32).rearrange("p (n u) -> p n u", u=2), turned_back[:].rearrange("p u n -> p n u")
            )

        def make_lo_from_words(q):
            nc.vector.tensor_tensor(
                packed_walk(lo_slots[q], VECTOR_RUN),
                rows_walk(wv_rows[q], VECTOR_RUN),
                rows_walk(hi_words[q], VECTOR_RUN),
                ALU.add,
            )

        def make_lo_kept(q):
            nc.vector.tensor_tensor(
                packed_walk(lo_slots[q][:, 0 : KEPT * PACK], VECTOR_RUN),
                rows_walk(wv_rows[q][:, :, 0:KEPT], VECTOR_RUN),
                packed_walk(hi_slots[q][:, 0 : KEPT * PACK], VECTOR_RUN),
                ALU.subtract,
            )

        def make_lo_on_pool(q):
            nc.gpsimd.tensor_tensor(
                lo_slots[q][:, KEPT * PACK :].rearrange("p (n t) -> p n t", t=PACK),
                wv_rows[q][:, :, KEPT:].rearrange("p t n -> p n t"),
                hi_slots[q][:, KEPT * PACK :].rearrange("p (n t) -> p n t", t=PACK),
                ALU.subtract,
            )

        def key_scales(a, h, count=1):
            if (a, h) == (1, 1):
                return val_plane[(1, 0)][SCALE_ROWS:P, 0:P]
            at = (HALVES * a + h) * P
            return key_plane[:, at : at + count * P]

        def quantise(codes, scales, values):
            nc.vector.quantize_mx(out=codes.bitcast(FP8X4), scales=scales, in_=values)

        def quantise_val(q):
            quantise(val_codes[q][:], val_plane[q][:], val[q][:])

        def mx_pass(acc, a, codes, scales, words, j0, j1, start, stop):
            nc.tensor.matmul_mx(
                out=acc,
                lhsT=codes.bitcast(FP8X4),
                lhsT_scale=scales,
                rhs=words.bitcast(FP8X4),
                rhs_scale=picked_plane[SCALE_ROWS * a : P, j0:j1],
                start=start,
                stop=stop,
            )

        def ke_pass(a, h, b):
            codes = key_codes[a][:, h * P : (h + 1) * P]
            mx_pass(ke[h][b], a, codes, key_scales(a, h), picked[(a, b)], b * PART, (b + 1) * PART, a == 0, a == PASSES - 1)

        def ve_pass(q, s, b, start, stop):
            cols = slice(s * P, (s + 1) * P)
            codes = val_codes[q][:, cols]
            mx_pass(ve[q[1]][b], q[0], codes, val_plane[q][:, cols], picked[(q[0], b)], b * PART, (b + 1) * PART, start, stop)

        def ve_last(codes, s, b, stop):
            scales = val_plane[(1, 1)][:, s * P : (s + 1) * P]
            mx_pass(ve[1][b], 1, codes, scales, picked[(1, b)], b * PART, (b + 1) * PART, False, stop)

        def make_gate(h, b):
            nc.vector.tensor_tensor(z[h][:, part(b)], st_sb[h][:, part(b)], ke[h][b], ALU.mult)
            nc.scalar.activation(gate[h][b][:], z[h][:, part(b)], ACT.Tanh)

        def apply_gate(h, b):
            nc.vector.tensor_tensor(prod[h][:, part(b)], gate[h][b][:], ve[h][b], ALU.mult)

        def add_record_and_store(h, j0, j1):
            nc.vector.tensor_tensor(res[h][:, j0:j1], r_sb[h][:].indirect(entries(j0, j1)), prod[h][:, j0:j1], ALU.add)
            nc.sync.dma_start(out[h * P : (h + 1) * P, j0:j1], res[h][:, j0:j1])

        nc.vector.memset(tab_plane[:].bitcast(I32), 0)

        make_identity_on_vector()
        load_weight(wv_raw[0][:], wv, 0, 0, N)
        nc.sync.dma_start(offsets[:], offs)
        load_scales()
        load_weight(wv_raw[1][:], wv, 1, 0, N)
        load_words(0)
        for a in range(PASSES):
            load_weight(wk_raw[a][:], wk, a, 0, N)
        load_words(1)
        for h in range(HALVES):
            nc.sync.dma_start(st_sb[h][:], st[h * P : (h + 1) * P, :])
        for h in range(HALVES):
            nc.sync.dma_start(r_sb[h][:], rT[h * P : (h + 1) * P, :])

        mask_words((0, 1), 0, 2)
        mask_words((0, 0), 0, PACK)
        mask_words((0, 1), 2, PACK)
        for h in range(HALVES):
            cast_negated(hi_slots[(0, h)], hi_words[(0, h)])
        make_lo_by_transposes((0, 1))
        copy_top(top_last[:], wv_raw[1][:])
        fetch_lo((0, 1))
        cast(key0[:], wk_raw[0][:])
        for h in range(HALVES):
            cast(key1[h], wk_rows[(1, h)])
        make_lo_from_words((0, 0))
        gather_scales()
        quantise_val((0, 0))
        for b in range(2):
            gather_words(picked[(0, b)], 0, b * PART, (b + 1) * PART)
            for s in range(2):
                ve_pass((0, 0), s, b, s == 0, False)
        for h in range(HALVES):
            mask_top((1, h))
        quantise_val((0, 1))
        for b in range(2):
            for s in range(2):
                ve_pass((0, 1), s, b, s == 0, False)
        make_lo((1, 0))
        make_lo_kept((1, 1))
        quantise(key_codes[0][:], key_scales(0, 0, HALVES), key0[:])
        ke.append([ps.tile([P, PART], F32, name=f"ke1{b}", tag=tag)[:] for b, tag in enumerate(("bank_a", "bank_b"))])
        for h in range(HALVES):
            for b in range(2):
                ke_pass(0, h, b)
        val_codes[(1, 0)] = tile("val_codes10", [P, 2 * P], U32, tag="wk_raw0")
        quantise_val((1, 0))
        gather_words(picked[(1, 0)], 1, 0, PART)
        quantise(key_codes[1][:, 0:P], key_scales(1, 0), key1[0])
        gather_words(picked[(1, 1)], 1, PART, J)
        quantise(key_codes[1][:, P : 2 * P], key_scales(1, 1), key1[1])
        hi_codes_last = tile("hi_codes_last", [P, P], U32, tag="wk_raw1")
        quantise(hi_codes_last[:], val_plane[(1, 1)][:, 0:P], hi_slots[(1, 1)])
        make_lo_on_pool((1, 1))
        for h in range(HALVES):
            for b in range(2):
                ke_pass(1, h, b)
        for b in range(2):
            for s in range(2):
                ve_pass((1, 0), s, b, False, s == 1)
        for b in range(2):
            ve_last(hi_codes_last[:], 0, b, False)
        for h in range(HALVES):
            for b in range(2):
                make_gate(h, b)
        for b in range(2):
            apply_gate(0, b)
        lo_codes_last = tile("lo_codes_last", [P, P], U32, tag="gate00")
        quantise(lo_codes_last[:], val_plane[(1, 1)][:, P : 2 * P], lo_slots[(1, 1)])
        for b in range(2):
            ve_last(lo_codes_last[:], 1, b, True)
        res[0] = tile("res0", [P, J], F32, tag="wv_raw1")
        for b in range(2):
            add_record_and_store(0, b * PART, (b + 1) * PART)
        for b in range(2):
            apply_gate(1, b)
        add_record_and_store(1, 0, PART)
        add_record_and_store(1, PART, LAST_CUT)
        add_record_and_store(1, LAST_CUT, J)
